import numpy as np
import ml_dtypes


def mxq(x, axis, fmt="e4m3"):
    dtype, down = {"e4m3": (ml_dtypes.float8_e4m3fn, 7), "e5m2": (ml_dtypes.float8_e5m2, 14)}[fmt]
    v = np.moveaxis(np.asarray(x, np.float32).astype(ml_dtypes.bfloat16).astype(np.float64), axis, -1)
    blocks = v.reshape(v.shape[:-1] + (-1, 32))
    amax = np.abs(blocks).max(-1, keepdims=True)
    byte = np.maximum(np.where(amax > 0, np.frexp(amax)[1] - 1 + 127, 0) - down, 1)
    scale = np.exp2(byte - 127.0)
    codes = (blocks / scale).astype(np.float32).astype(dtype).astype(np.float64)
    return np.moveaxis((codes * scale).reshape(v.shape), -1, axis)


WIDE = False


def mx_kscale(k):
    if not WIDE:
        return np.ones(k)
    levels = np.array([10, -10, 5, -5, 0])
    if k % 512:
        return np.exp2(np.random.permutation(np.resize(levels, k // 32))).repeat(32)
    a = np.empty((k // 512, 16))
    for p in range(k // 512):
        a[p, :8] = np.random.permutation(np.resize(levels, 8))
        for g in range(8):
            far = levels[np.abs(levels - a[p, g]) >= 10]
            a[p, g + 8] = far[np.random.randint(len(far))]
    return np.exp2(a.ravel()).repeat(32)


BF16 = ml_dtypes.bfloat16


def bf(x):
    return np.asarray(x, np.float32).astype(BF16)


def f64(x):
    return np.asarray(x).astype(np.float64)


T, D, R, C = 1024, 2048, 512, 1024


def draw0():
    s, u = mx_kscale(D), mx_kscale(T)
    x = np.random.standard_normal((T, D)) * s * u[:, None]
    w_key = np.random.standard_normal((D, R)) / np.sqrt(D) / s[:, None]
    w_value = np.random.standard_normal((D, C)) / np.sqrt(D) / s[:, None]
    pos = 0.5 * np.random.standard_normal((T, R)) * u[:, None]
    emphasis = (0.5 + np.random.random(T)) / T ** 0.25 / u ** 2
    return {"x": bf(x),
            "w_key": bf(w_key),
            "w_value": bf(w_value),
            "pos": bf(pos),
            "emphasis": bf(emphasis)}


def core(x, w_key, w_value, pos, emphasis):
    xq = mxq(f64(x), 1, "e4m3")
    key = np.maximum((xq @ mxq(f64(w_key), 0, "e4m3")) + f64(pos), 0)
    value = (xq @ mxq(f64(w_value), 0, "e4m3")) * f64(emphasis)[:, None]
    return mxq(key, 0, "e4m3").T @ mxq(value, 0, "e4m3")


def e4m3fn_bytes(y):
    return np.clip(np.asarray(y, np.float64), -448.0, 448.0).astype(np.float32).astype(ml_dtypes.float8_e4m3fn).view(np.uint8)


def e4m3fn_values(b):
    return np.asarray(b, np.uint8).view(ml_dtypes.float8_e4m3fn).astype(np.float64)


def setup_inputs():
    d = draw0()
    x0 = np.asarray(d['w_value']).astype(np.float64)
    s = (np.max(np.abs(x0), axis=(1,), keepdims=True) / 448.0).astype(np.float32)
    out = {}
    for k, v in d.items():
        if k == 'w_value':
            out['w_value_bytes'] = e4m3fn_bytes(x0 / s.astype(np.float64))
            out['w_value_scale'] = s
        else:
            out[k] = v
    return out


def reference(x, w_key, w_value_bytes, w_value_scale, pos, emphasis):
    return core(x, w_key, e4m3fn_values(w_value_bytes) * w_value_scale.astype(np.float64), pos, emphasis)

@@ -1,0 +1,419 @@
+from contextlib import ExitStack
+
+import concourse.mybir as mybir
+from concourse.masks import make_identity
+
+T, D, R, C = 1024, 2048, 512, 1024
+FLOPS = 2 * T * D * (R + C) + 2 * T * R * C
+
+F32 = mybir.dt.float32
+BF16 = mybir.dt.bfloat16
+U32 = mybir.dt.uint32
+U8 = mybir.dt.uint8
+FP8 = mybir.dt.float8_e4m3fn
+FP8X4 = mybir.dt.float8_e4m3fn_x4
+ALU = mybir.AluOpType
+COPY = mybir.ActivationFunctionType.Copy
+RELU = mybir.ActivationFunctionType.Relu
+
+P = 128
+PACK = 4
+K_PASS = P * PACK
+D_PASSES = D // K_PASS
+GROUPS = T // K_PASS
+HALF = 512
+
+
+def tile_text_image_memory_bridge_s7_kernel(
+    tc, x, w_key, w_value_bytes, w_value_scale, pos, emphasis, out
+):
+    nc = tc.nc
+    with ExitStack() as ctx:
+        raw = ctx.enter_context(tc.tile_pool(name="raw", bufs=1))
+        work = ctx.enter_context(tc.tile_pool(name="work", bufs=4))
+        keep = ctx.enter_context(tc.tile_pool(name="keep", bufs=1))
+        psum = ctx.enter_context(tc.psum_pool(name="psum", bufs=1))
+        ctx.enter_context(tc.manual_schedule())
+
+        x_v = x.rearrange("(g m t) k -> g t m k", g=GROUPS, t=PACK)
+        wk_v = w_key.rearrange("(g p t) n -> g p t n", p=P, t=PACK)
+        wv_v = w_value_bytes.rearrange("(g p t) n -> g p t n", p=P, t=PACK)
+        pos_v = pos.rearrange("(g p t) n -> g p t n", p=P, t=PACK)
+
+        ident = keep.tile([P, P], F32, name="ident")
+        make_identity(nc, ident[:])
+
+        x_raw, wk_raw, wv_raw, pos_raw = {}, {}, {}, {}
+
+        def load_x(i):
+            tile = raw.tile([P, D], BF16, name="xraw", tag="xraw", bufs=8, align_bytes=64)
+            nc.sync.dma_start(out=tile[:], in_=x_v[i // PACK, i % PACK])
+            x_raw[i] = tile
+
+        def load_wk(g):
+            tile = raw.tile([P, PACK, R], BF16, name="wkraw", tag="wkraw", bufs=4, align_bytes=64)
+            nc.sync.dma_start(out=tile[:], in_=wk_v[g])
+            wk_raw[g] = tile
+
+        def load_wv(g):
+            tile = raw.tile([P, PACK, C], U8, name="wvraw", tag="wvraw", bufs=4, align_bytes=64)
+            nc.sync.dma_start(out=tile[:], in_=wv_v[g])
+            wv_raw[g] = tile
+
+        def load_pos(g):
+            tile = raw.tile([P, PACK, R], BF16, name="posraw", tag="posraw", bufs=2, align_bytes=64)
+            nc.sync.dma_start(out=tile[:], in_=pos_v[g])
+            pos_raw[g] = tile
+
+
+        wv_scale = keep.tile([P, D_PASSES, PACK], F32, name="wvscale")
+        nc.scalar.dma_start(
+            out=wv_scale[:], in_=w_value_scale.rearrange("(g p t) o -> p g (t o)", p=P, t=PACK)
+        )
+        emph_bf = keep.tile([P, GROUPS, PACK], BF16, name="emphbf")
+        nc.scalar.dma_start(out=emph_bf[:], in_=emphasis.rearrange("(g p t) -> p g t", p=P, t=PACK))
+        for name in "k0 x0 k1 x1 v0 x2 k2 x3 k3 x4 v1 p0 x5 x6 x7 v2 p1 v3".split():
+            {"k": load_wk, "x": load_x, "v": load_wv, "p": load_pos}[name[0]](int(name[1]))
+
+        emph = keep.tile([P, GROUPS, PACK], F32, name="emph")
+
+        codes, scales, ils, banks = {}, {}, {}, {}
+
+        def quantize(key):
+            src = ils[key][:]
+            width = src.shape[1] // PACK
+            c = keep.tile([P, width], U32, name="c_" + key, align_bytes=64)
+            s = keep.tile([P, width], U8, name="s_" + key, align_bytes=64)
+            nc.vector.quantize_mx(out=c[:].bitcast(FP8X4), scales=s[:], in_=src)
+            codes[key], scales[key] = c, s
+
+        def il_tile(key):
+            ils[key] = work.tile([P, K_PASS * PACK], BF16, name="il", tag="il", bufs=8, align_bytes=64)
+            return ils[key]
+
+        def fan(dst):
+            return dst[:].rearrange("p (c i t) -> p c t i", i=4, t=PACK)
+
+        def rows(src):
+            return src[:].rearrange("p t (c i) -> p c t i", i=4)
+
+        def mm(bank, lhs, lcol, rhs, rcol, n, start, stop):
+            nc.tensor.matmul_mx(
+                out=bank,
+                lhsT=codes[lhs][:, lcol : lcol + P].bitcast(FP8X4),
+                lhsT_scale=scales[lhs][:, lcol : lcol + P],
+                rhs=codes[rhs][:, rcol : rcol + n].bitcast(FP8X4),
+                rhs_scale=scales[rhs][:, rcol : rcol + n],
+                start=start,
+                stop=stop,
+            )
+
+        def bank_tile(b):
+            return psum.tile([P, 512], F32, name="bank", tag="bank%d" % b, bufs=1)
+
+        def xT(i):
+            words = x_raw[i][:].bitcast(F32)
+            for gg in range(2):
+                bank = bank_tile((2 * i + gg) % 4)
+                xt = bank[:].rearrange("p (g u r) -> p g u r", g=2, u=2)
+                for j in range(2):
+                    base = 256 * (2 * gg + j)
+                    for u in range(2):
+                        nc.tensor.transpose(xt[:, j, u, :], words[:, base + u : base + 256 : 2], ident[:])
+                banks["x%d%d" % (i, gg)] = bank
+
+        def xC(i):
+            il = il_tile("x%d" % i)
+            for gg in range(2):
+                dst = il[:, 1024 * gg : 1024 * (gg + 1)].bitcast(F32)
+                nc.scalar.copy(
+                    out=dst.rearrange("p (g r u) -> p g r u", g=2, u=2),
+                    in_=banks["x%d%d" % (i, gg)][:].rearrange("p (g u r) -> p g r u", g=2, u=2),
+                )
+
+        def xQ(i):
+            quantize("x%d" % i)
+
+        def wkI(g):
+            nc.vector.tensor_copy(out=fan(il_tile("wk%d" % g)), in_=rows(wk_raw[g]))
+
+        def wkQ(g):
+            quantize("wk%d" % g)
+
+        wide = {}
+
+        def wvW(g, h, t):
+            if t == 0:
+                wide[g, h] = work.tile([P, PACK, HALF], BF16, name="wide", tag="wide", bufs=4, align_bytes=64)
+            nc.scalar.activation(
+                out=wide[g, h][:, t, :],
+                in_=wv_raw[g][:, t, HALF * h : HALF * (h + 1)].bitcast(FP8),
+                func=COPY,
+                scale=wv_scale[:, g, t : t + 1],
+            )
+
+        def wvI(g, h):
+            nc.vector.tensor_copy(out=fan(il_tile("wv%d_%d" % (g, h))), in_=rows(wide[g, h]))
+
+        def wvQ(g, h):
+            quantize("wv%d_%d" % (g, h))
+
+        def kM(i, k):
+            if k == 0:
+                banks["k%d" % i] = bank_tile(4 + i % 4)
+            mm(banks["k%d" % i][:], "x%d" % i, P * k, "wk%d" % k, 0, 512, k == 0, k == D_PASSES - 1)
+
+        def kN(i):
+            for cb in range(4):
+                if i % 4 == 0:
+                    banks["n%d%d" % (i // 4, cb)] = bank_tile(4 + cb)
+                bank = banks["n%d%d" % (i // 4, cb)]
+                for k in range(4):
+                    mm(
+                        bank[:, P * (i % 4) : P * (i % 4 + 1)],
+                        "x%d" % i, P * k, "wk%d" % k, P * cb, P, k == 0, k == D_PASSES - 1,
+                    )
+
+        def kAN(g, cb):
+            if cb == 0:
+                key_raw[g] = work.tile([P, R * PACK], BF16, name="kraw", tag="kraw", bufs=2, align_bytes=64)
+            nc.vector.tensor_tensor(
+                out=key_raw[g][:, 512 * cb : 512 * (cb + 1)].rearrange("p (c t) -> p c t", t=PACK),
+                in0=banks["n%d%d" % (g, cb)][:].rearrange("p (t c) -> p c t", t=PACK),
+                in1=pos_raw[g][:, :, P * cb : P * (cb + 1)].rearrange("p t c -> p c t"),
+                op=ALU.add,
+            )
+
+        def kR(g):
+            nc.vector.tensor_scalar(
+                out=il_tile("key%d" % g)[:], in0=key_raw[g][:], scalar1=0.0, scalar2=None, op0=ALU.max
+            )
+
+        key_raw, val_raw = {}, {}
+
+        def kA(i):
+            g, t = divmod(i, PACK)
+            if t == 0:
+                key_raw[g] = work.tile([P, PACK, R], BF16, name="kraw", tag="kraw", bufs=2, align_bytes=64)
+            nc.vector.tensor_tensor(
+                out=key_raw[g][:, t, :], in0=banks["k%d" % i][:], in1=pos_raw[g][:, t, :], op=ALU.add
+            )
+
+        def kI(g):
+            il = il_tile("key%d" % g)
+            if g == 1:
+                nc.scalar.activation(out=fan(il), in_=rows(key_raw[g]), func=RELU)
+            else:
+                nc.vector.tensor_scalar(
+                    out=fan(il), in0=rows(key_raw[g]), scalar1=0.0, scalar2=None, op0=ALU.max
+                )
+
+        def kQ(g):
+            quantize("key%d" % g)
+
+        BLK = {"a": (0, 512), "b": (512, 256), "c": (768, 256)}
+
+        def vM(i, blk, k, bk=None):
+            c0, n = BLK[blk]
+            if k == 0:
+                banks["v%d%s" % (i, blk)] = bank_tile(i if bk is None else bk)
+            mm(
+                banks["v%d%s" % (i, blk)][:, :n], "x%d" % i, P * k,
+                "wv%d_%d" % (k, c0 // HALF), c0 % HALF, n, k == 0, k == D_PASSES - 1,
+            )
+
+        def vO(i, blk, eng="S"):
+            g, t = divmod(i, PACK)
+            n = BLK[blk][1]
+            if t == 0:
+                val_raw[g, blk] = work.tile([P, PACK, n], BF16, name="vraw", tag="vraw%d" % n, bufs=3, align_bytes=64)
+            if eng == "S":
+                nc.scalar.activation(
+                    out=val_raw[g, blk][:, t, :], in_=banks["v%d%s" % (i, blk)][:, :n],
+                    func=COPY, scale=emph[:, g, t : t + 1],
+                )
+            else:
+                nc.vector.tensor_scalar(
+                    out=val_raw[g, blk][:, t, :], in0=banks["v%d%s" % (i, blk)][:, :n],
+                    scalar1=emph[:, g, t : t + 1], scalar2=None, op0=ALU.mult,
+                )
+
+        def vI(g, blk):
+            n = BLK[blk][1]
+            il = work.tile([P, n * PACK], BF16, name="il", tag="il", bufs=8, align_bytes=64)
+            ils["val%d%s" % (g, blk)] = il
+            nc.vector.tensor_copy(out=fan(il), in_=rows(val_raw[g, blk]))
+
+        def vQ(g, blk):
+            quantize("val%d%s" % (g, blk))
+
+        def oM(m, blk, g, bk=None):
+            n = BLK[blk][1]
+            if g == 0:
+                banks["o%d%s" % (m, blk)] = bank_tile(bk)
+            mm(banks["o%d%s" % (m, blk)][:, :n], "key%d" % g, P * m, "val%d%s" % (g, blk), 0, n, g == 0, g == GROUPS - 1)
+
+        def oC(m, blk, eng=None):
+            c0, n = BLK[blk]
+            res = work.tile([P, n], F32, name="res", tag="res%d" % n, bufs=8 if n == 256 else 4)
+            if (eng or "SV"[m % 2]) == "S":
+                nc.scalar.copy(out=res[:], in_=banks["o%d%s" % (m, blk)][:, :n])
+            else:
+                nc.vector.tensor_copy(out=res[:], in_=banks["o%d%s" % (m, blk)][:, :n])
+            nc.sync.dma_start(out=out[P * m : P * (m + 1), c0 : c0 + n], in_=res[:])
+
+        quarters = [(g, h, t) for h in range(2) for g in range(4) for t in range(PACK)]
+        quarters = [(0, h, t) for h in range(2) for t in range(PACK)] + [
+            (g, h, t) for h in range(2) for g in range(1, 4) for t in range(PACK)
+        ]
+
+        def widen(n):
+            for _ in range(n):
+                wvW(*quarters.pop(0))
+
+        def wave(i):
+            for k in range(i):
+                kM(i, k)
+            for j in range(i + 1):
+                kM(j, i)
+
+        xT(0)
+        wkI(0)
+        wkI(1)
+        nc.vector.tensor_copy(out=emph[:], in_=emph_bf[:])
+        xC(0)
+        wkQ(0)
+        xQ(0)
+        xT(1)
+        xC(1)
+        wkQ(1)
+        xQ(1)
+        wave(0)
+        xT(2)
+        widen(2)
+        xC(2)
+        wave(1)
+        wkI(2)
+        xQ(2)
+        wkQ(2)
+        widen(2)
+        xT(3)
+        xC(3)
+        wave(2)
+        wkI(3)
+        xQ(3)
+        wkQ(3)
+        wvI(0, 0)
+        widen(2)
+        xT(4)
+        xC(4)
+        wave(3)
+        xQ(4)
+        wvQ(0, 0)
+        widen(2)
+        xT(5)
+        xC(5)
+        kA(0)
+        kA(1)
+        xQ(5)
+        for k in range(4):
+            kM(4, k)
+        wvI(0, 1)
+        kA(2)
+        kA(3)
+        widen(2)
+        xT(6)
+        xC(6)
+        for k in range(4):
+            kM(5, k)
+        xQ(6)
+        wvQ(0, 1)
+        widen(2)
+        xT(7)
+        xC(7)
+        for k in range(4):
+            kM(6, k)
+        wvI(1, 0)
+        xQ(7)
+        wvQ(1, 0)
+        kA(4)
+        kA(5)
+        for k in range(4):
+            kM(7, k)
+        widen(4)
+        kA(6)
+        wvI(2, 0)
+        kA(7)
+        wvQ(2, 0)
+        widen(4)
+        wvI(3, 0)
+        for k in range(3):
+            for i in range(8):
+                vM(i, "a", k)
+        widen(4)
+        wvI(1, 1)
+        wvQ(3, 0)
+        for i in range(8):
+            vM(i, "a", 3)
+        widen(4)
+        wvI(2, 1)
+        wvQ(1, 1)
+        widen(4)
+        for i in range(4):
+            vO(i, "a")
+        wvI(3, 1)
+        wvQ(2, 1)
+        kI(0)
+        wvQ(3, 1)
+        for i in range(4, 8):
+            vO(i, "a")
+        vI(0, "a")
+        kQ(0)
+        for k in range(4):
+            for i in range(4):
+                vM(i, "b", k)
+        kI(1)
+        for i in range(4):
+            vO(i, "b")
+        vI(1, "a")
+        vQ(0, "a")
+        for i in range(4, 8):
+            for k in range(4):
+                vM(i, "b", k)
+        vQ(1, "a")
+        vI(0, "b")
+        kQ(1)
+        for i in range(4, 8):
+            vO(i, "b")
+        for i in range(4):
+            for k in range(4):
+                vM(i, "c", k)
+        vQ(0, "b")
+        vI(1, "b")
+        for i in range(4):
+            vO(i, "c")
+        for i in range(4, 8):
+            for k in range(4):
+                vM(i, "c", k)
+        vQ(1, "b")
+        vI(0, "c")
+        for i in range(4, 8):
+            vO(i, "c", "SVSV"[i - 4])
+        for m in range(4):
+            for g in range(2):
+                oM(m, "a", g, m)
+        vQ(0, "c")
+        vI(1, "c")
+        for m in range(4):
+            oC(m, "a")
+        vQ(1, "c")
+        for m in range(4):
+            for g in range(2):
+                oM(m, "b", g, 4 + m)
+        for m in range(4):
+            oC(m, "b")
+        for m in range(4):
+            oM(m, "c", 0, m)
+        for m in range(4):
+            oM(m, "c", 1)
+            oC(m, "c")

@@ -14,7 +14,6 @@ FP8 = mybir.dt.float8_e4m3fn
 FP8X4 = mybir.dt.float8_e4m3fn_x4
 ALU = mybir.AluOpType
 COPY = mybir.ActivationFunctionType.Copy
-RELU = mybir.ActivationFunctionType.Relu
 
 P = 128
 PACK = 4
@@ -22,6 +21,21 @@ K_PASS = P * PACK
 D_PASSES = D // K_PASS
 GROUPS = T // K_PASS
 HALF = 512
+BLOCKS = {"a": (0, 512), "b": (512, 256), "c": (768, 256)}
+
+LOADS = "wv0a wv0b wv2 x0 wv3 x3 x5 x4 x6 x2 wv1 x1 x7 wk3 pos0 wk2 pos1 wk1 wk0"
+ORDER = """
+    wvW000.S wvW010.V wvW001.V wvI00.V wvW011.S wvW210.V wvW200.S wvW211.V wvQ00.V xC00.S wvW311.V
+    wvW301.V wvW201.S wvI20.V wvW300.S wvI30.V wvQ20.V wvQ30.V xC31.S xC30.S xC40.S xC41.S xC60.S
+    xC61.S xC20.S xQ3.V xQ4.V xQ6.V wvW100.V wvW310.V wvW101.S wvI10.V xC01.S xQ0.V xC51.S xC10.S
+    xC21.S xC70.S xC71.S xC11.S xC50.S wvW111.S wvQ10.V vO4a.S vO0a.S wkI3.V xQ2.V wvW110.S xQ1.V
+    vO1a.S xQ7.V vO7a.S wkI2.V wvI21.S vO3a.S wkQ3.V wkQ2.V wkI1.V xQ5.V wkQ1.V wkI0.V wkQ0.V kA0.V
+    kA1.V kA3.V kA2.V kA1n0.V wvI11.S wvQ11.V kA1n1.V wvQ21.V wvI01.S wvQ01.V vO6a.S wvI31.S
+    kA1n2.V vO2a.V vI0a.S kA1n3.V vO5a.V wvQ31.V vO1b.S vO0b.S vO7b.S vO3b.S vO4b.S vO6b.S vO2b.S
+    vO5b.S vO0c.S vO1c.S vI1b.S vO3c.S vO5c.S vO6c.S vO4c.S vI1a.V vQ1a.V vQ0a.V vO7c.S kI1.V kQ1.V
+    kI0.V kQ0.V oC0a.S oC3a.S oC2a.S vO2c.V vI0c.V vI0b.V vQ0b.V oC1a.V vQ1b.V oC0b.S oC3b.S oC1b.S
+    oC2b.S vQ0c.V vI1c.V vQ1c.V oC0c.V oC1c.S oC3c.V oC2c.V
+"""
 
 
 def tile_text_image_memory_bridge_s7_kernel(
@@ -29,7 +43,6 @@ def tile_text_image_memory_bridge_s7_kernel(
 ):
     nc = tc.nc
     with ExitStack() as ctx:
-        raw = ctx.enter_context(tc.tile_pool(name="raw", bufs=1))
         work = ctx.enter_context(tc.tile_pool(name="work", bufs=4))
         keep = ctx.enter_context(tc.tile_pool(name="keep", bufs=1))
         psum = ctx.enter_context(tc.psum_pool(name="psum", bufs=1))
@@ -40,44 +53,45 @@ def tile_text_image_memory_bridge_s7_kernel(
         wv_v = w_value_bytes.rearrange("(g p t) n -> g p t n", p=P, t=PACK)
         pos_v = pos.rearrange("(g p t) n -> g p t n", p=P, t=PACK)
 
-        ident = keep.tile([P, P], F32, name="ident")
-        make_identity(nc, ident[:])
+        raws = {}
 
-        x_raw, wk_raw, wv_raw, pos_raw = {}, {}, {}, {}
+        def raw_tile(kind, n):
+            shape, dtype = {
+                "x": ([P, D], BF16),
+                "wk": ([P, PACK, R], BF16),
+                "wv": ([P, PACK, C], U8),
+                "pos": ([P, PACK, R], BF16),
+            }[kind]
+            raws[kind, n] = work.tile(shape, dtype, name=kind + "raw", tag="pos" if kind == "pos" else "t4", bufs=2 if kind == "pos" else 32, align_bytes=64)
+            return raws[kind, n]
 
-        def load_x(i):
-            tile = raw.tile([P, D], BF16, name="xraw", tag="xraw", bufs=8, align_bytes=64)
-            nc.sync.dma_start(out=tile[:], in_=x_v[i // PACK, i % PACK])
-            x_raw[i] = tile
+        def load(word):
+            stem = word[:-1] if word[-1] in "ab" else word
+            kind, n = stem[:-1], int(stem[-1])
+            if word[-1] == "a":
+                nc.sync.dma_start(out=raw_tile(kind, n)[:, 0:2, :], in_=wv_v[n][:, 0:2, :])
+            elif word[-1] == "b":
+                nc.sync.dma_start(out=raws[kind, n][:, 2:4, :], in_=wv_v[n][:, 2:4, :])
+            else:
+                view = x_v[n // PACK, n % PACK] if kind == "x" else {"wk": wk_v, "wv": wv_v, "pos": pos_v}[kind][n]
+                nc.sync.dma_start(out=raw_tile(kind, n)[:], in_=view)
 
-        def load_wk(g):
-            tile = raw.tile([P, PACK, R], BF16, name="wkraw", tag="wkraw", bufs=4, align_bytes=64)
-            nc.sync.dma_start(out=tile[:], in_=wk_v[g])
-            wk_raw[g] = tile
-
-        def load_wv(g):
-            tile = raw.tile([P, PACK, C], U8, name="wvraw", tag="wvraw", bufs=4, align_bytes=64)
-            nc.sync.dma_start(out=tile[:], in_=wv_v[g])
-            wv_raw[g] = tile
-
-        def load_pos(g):
-            tile = raw.tile([P, PACK, R], BF16, name="posraw", tag="posraw", bufs=2, align_bytes=64)
-            nc.sync.dma_start(out=tile[:], in_=pos_v[g])
-            pos_raw[g] = tile
-
-
+        words = LOADS.split()
+        load(words[0])
+        load(words[1])
         wv_scale = keep.tile([P, D_PASSES, PACK], F32, name="wvscale")
         nc.scalar.dma_start(
             out=wv_scale[:], in_=w_value_scale.rearrange("(g p t) o -> p g (t o)", p=P, t=PACK)
         )
         emph_bf = keep.tile([P, GROUPS, PACK], BF16, name="emphbf")
         nc.scalar.dma_start(out=emph_bf[:], in_=emphasis.rearrange("(g p t) -> p g t", p=P, t=PACK))
-        for name in "k0 x0 k1 x1 v0 x2 k2 x3 k3 x4 v1 p0 x5 x6 x7 v2 p1 v3".split():
-            {"k": load_wk, "x": load_x, "v": load_wv, "p": load_pos}[name[0]](int(name[1]))
-
+        for word in words[2:]:
+            load(word)
+        ident = keep.tile([P, P], F32, name="ident")
+        make_identity(nc, ident[:])
         emph = keep.tile([P, GROUPS, PACK], F32, name="emph")
 
-        codes, scales, ils, banks = {}, {}, {}, {}
+        codes, scales, ils, rows, banks = {}, {}, {}, {}, {}
 
         def quantize(key):
             src = ils[key][:]
@@ -87,15 +101,28 @@ def tile_text_image_memory_bridge_s7_kernel(
             nc.vector.quantize_mx(out=c[:].bitcast(FP8X4), scales=s[:], in_=src)
             codes[key], scales[key] = c, s
 
-        def il_tile(key):
-            ils[key] = work.tile([P, K_PASS * PACK], BF16, name="il", tag="il", bufs=8, align_bytes=64)
+        def il_tile(key, n):
+            ils[key] = work.tile(
+                [P, n * PACK], BF16, name="il", tag="t4" if n == 512 else "t2",
+                bufs=32 if n == 512 else 8, align_bytes=64
+            )
             return ils[key]
 
-        def fan(dst):
-            return dst[:].rearrange("p (c i t) -> p c t i", i=4, t=PACK)
+        def interleave(key, src, engine, n=512, relu=False):
+            dst = il_tile(key, n)[:].rearrange("p (c i t) -> p c t i", i=4, t=PACK)
+            src = src[:].rearrange("p t (c i) -> p c t i", i=4)
+            if relu:
+                nc.vector.tensor_scalar(out=dst, in0=src, scalar1=0.0, scalar2=None, op0=ALU.max)
+            elif engine == "S":
+                nc.scalar.copy(out=dst, in_=src)
+            else:
+                nc.vector.tensor_copy(out=dst, in_=src)
 
-        def rows(src):
-            return src[:].rearrange("p t (c i) -> p c t i", i=4)
+        def scaled(dst, src, scale, engine):
+            if engine == "S":
+                nc.scalar.activation(out=dst, in_=src, func=COPY, scale=scale)
+            else:
+                nc.vector.tensor_scalar(out=dst, in0=src, scalar1=scale, scalar2=None, op0=ALU.mult)
 
         def mm(bank, lhs, lcol, rhs, rcol, n, start, stop):
             nc.tensor.matmul_mx(
@@ -108,312 +135,215 @@ def tile_text_image_memory_bridge_s7_kernel(
                 stop=stop,
             )
 
-        def bank_tile(b):
-            return psum.tile([P, 512], F32, name="bank", tag="bank%d" % b, bufs=1)
+        tensor_work = {}
 
-        def xT(i):
-            words = x_raw[i][:].bitcast(F32)
-            for gg in range(2):
-                bank = bank_tile((2 * i + gg) % 4)
+        def transposes(i, q):
+            def run(bank):
+                w = raws["x", i][:].bitcast(F32)
                 xt = bank[:].rearrange("p (g u r) -> p g u r", g=2, u=2)
                 for j in range(2):
-                    base = 256 * (2 * gg + j)
+                    base = 256 * (2 * q + j)
                     for u in range(2):
-                        nc.tensor.transpose(xt[:, j, u, :], words[:, base + u : base + 256 : 2], ident[:])
-                banks["x%d%d" % (i, gg)] = bank
+                        nc.tensor.transpose(xt[:, j, u, :], w[:, base + u : base + 256 : 2], ident[:])
+            return run
 
-        def xC(i):
-            il = il_tile("x%d" % i)
-            for gg in range(2):
-                dst = il[:, 1024 * gg : 1024 * (gg + 1)].bitcast(F32)
-                nc.scalar.copy(
-                    out=dst.rearrange("p (g r u) -> p g r u", g=2, u=2),
-                    in_=banks["x%d%d" % (i, gg)][:].rearrange("p (g u r) -> p g r u", g=2, u=2),
-                )
+        count = {}
 
-        def xQ(i):
-            quantize("x%d" % i)
+        def pass_of(key, total, cols, lhs, lcol, rhs, rcol, n):
+            def run(bank):
+                done = count.get(key, 0)
+                count[key] = done + 1
+                mm(bank[:, cols : cols + n], lhs, lcol, rhs, rcol, n, done == 0, done == total - 1)
+            return run
 
-        def wkI(g):
-            nc.vector.tensor_copy(out=fan(il_tile("wk%d" % g)), in_=rows(wk_raw[g]))
-
-        def wkQ(g):
-            quantize("wk%d" % g)
-
-        wide = {}
-
-        def wvW(g, h, t):
-            if t == 0:
-                wide[g, h] = work.tile([P, PACK, HALF], BF16, name="wide", tag="wide", bufs=4, align_bytes=64)
-            nc.scalar.activation(
-                out=wide[g, h][:, t, :],
-                in_=wv_raw[g][:, t, HALF * h : HALF * (h + 1)].bitcast(FP8),
-                func=COPY,
-                scale=wv_scale[:, g, t : t + 1],
-            )
-
-        def wvI(g, h):
-            nc.vector.tensor_copy(out=fan(il_tile("wv%d_%d" % (g, h))), in_=rows(wide[g, h]))
-
-        def wvQ(g, h):
-            quantize("wv%d_%d" % (g, h))
-
-        def kM(i, k):
-            if k == 0:
-                banks["k%d" % i] = bank_tile(4 + i % 4)
-            mm(banks["k%d" % i][:], "x%d" % i, P * k, "wk%d" % k, 0, 512, k == 0, k == D_PASSES - 1)
-
-        def kN(i):
-            for cb in range(4):
-                if i % 4 == 0:
-                    banks["n%d%d" % (i // 4, cb)] = bank_tile(4 + cb)
-                bank = banks["n%d%d" % (i // 4, cb)]
-                for k in range(4):
+        def passes4(i, cb):
+            def run(bank):
+                for k in range(D_PASSES):
                     mm(
-                        bank[:, P * (i % 4) : P * (i % 4 + 1)],
+                        bank[:, P * (i % PACK) : P * (i % PACK + 1)],
                         "x%d" % i, P * k, "wk%d" % k, P * cb, P, k == 0, k == D_PASSES - 1,
                     )
+            return run
 
-        def kAN(g, cb):
-            if cb == 0:
-                key_raw[g] = work.tile([P, R * PACK], BF16, name="kraw", tag="kraw", bufs=2, align_bytes=64)
-            nc.vector.tensor_tensor(
-                out=key_raw[g][:, 512 * cb : 512 * (cb + 1)].rearrange("p (c t) -> p c t", t=PACK),
-                in0=banks["n%d%d" % (g, cb)][:].rearrange("p (t c) -> p c t", t=PACK),
-                in1=pos_raw[g][:, :, P * cb : P * (cb + 1)].rearrange("p t c -> p c t"),
-                op=ALU.add,
-            )
-
-        def kR(g):
-            nc.vector.tensor_scalar(
-                out=il_tile("key%d" % g)[:], in0=key_raw[g][:], scalar1=0.0, scalar2=None, op0=ALU.max
-            )
-
-        key_raw, val_raw = {}, {}
-
-        def kA(i):
-            g, t = divmod(i, PACK)
-            if t == 0:
-                key_raw[g] = work.tile([P, PACK, R], BF16, name="kraw", tag="kraw", bufs=2, align_bytes=64)
-            nc.vector.tensor_tensor(
-                out=key_raw[g][:, t, :], in0=banks["k%d" % i][:], in1=pos_raw[g][:, t, :], op=ALU.add
-            )
-
-        def kI(g):
-            il = il_tile("key%d" % g)
-            if g == 1:
-                nc.scalar.activation(out=fan(il), in_=rows(key_raw[g]), func=RELU)
-            else:
-                nc.vector.tensor_scalar(
-                    out=fan(il), in0=rows(key_raw[g]), scalar1=0.0, scalar2=None, op0=ALU.max
-                )
-
-        def kQ(g):
-            quantize("key%d" % g)
-
-        BLK = {"a": (0, 512), "b": (512, 256), "c": (768, 256)}
-
-        def vM(i, blk, k, bk=None):
-            c0, n = BLK[blk]
-            if k == 0:
-                banks["v%d%s" % (i, blk)] = bank_tile(i if bk is None else bk)
-            mm(
-                banks["v%d%s" % (i, blk)][:, :n], "x%d" % i, P * k,
-                "wv%d_%d" % (k, c0 // HALF), c0 % HALF, n, k == 0, k == D_PASSES - 1,
-            )
-
-        def vO(i, blk, eng="S"):
-            g, t = divmod(i, PACK)
-            n = BLK[blk][1]
-            if t == 0:
-                val_raw[g, blk] = work.tile([P, PACK, n], BF16, name="vraw", tag="vraw%d" % n, bufs=3, align_bytes=64)
-            if eng == "S":
-                nc.scalar.activation(
-                    out=val_raw[g, blk][:, t, :], in_=banks["v%d%s" % (i, blk)][:, :n],
-                    func=COPY, scale=emph[:, g, t : t + 1],
-                )
-            else:
-                nc.vector.tensor_scalar(
-                    out=val_raw[g, blk][:, t, :], in0=banks["v%d%s" % (i, blk)][:, :n],
-                    scalar1=emph[:, g, t : t + 1], scalar2=None, op0=ALU.mult,
-                )
-
-        def vI(g, blk):
-            n = BLK[blk][1]
-            il = work.tile([P, n * PACK], BF16, name="il", tag="il", bufs=8, align_bytes=64)
-            ils["val%d%s" % (g, blk)] = il
-            nc.vector.tensor_copy(out=fan(il), in_=rows(val_raw[g, blk]))
-
-        def vQ(g, blk):
-            quantize("val%d%s" % (g, blk))
-
-        def oM(m, blk, g, bk=None):
-            n = BLK[blk][1]
-            if g == 0:
-                banks["o%d%s" % (m, blk)] = bank_tile(bk)
-            mm(banks["o%d%s" % (m, blk)][:, :n], "key%d" % g, P * m, "val%d%s" % (g, blk), 0, n, g == 0, g == GROUPS - 1)
-
-        def oC(m, blk, eng=None):
-            c0, n = BLK[blk]
-            res = work.tile([P, n], F32, name="res", tag="res%d" % n, bufs=8 if n == 256 else 4)
-            if (eng or "SV"[m % 2]) == "S":
-                nc.scalar.copy(out=res[:], in_=banks["o%d%s" % (m, blk)][:, :n])
-            else:
-                nc.vector.tensor_copy(out=res[:], in_=banks["o%d%s" % (m, blk)][:, :n])
-            nc.sync.dma_start(out=out[P * m : P * (m + 1), c0 : c0 + n], in_=res[:])
-
-        quarters = [(g, h, t) for h in range(2) for g in range(4) for t in range(PACK)]
-        quarters = [(0, h, t) for h in range(2) for t in range(PACK)] + [
-            (g, h, t) for h in range(2) for g in range(1, 4) for t in range(PACK)
-        ]
-
-        def widen(n):
-            for _ in range(n):
-                wvW(*quarters.pop(0))
-
-        def wave(i):
-            for k in range(i):
-                kM(i, k)
-            for j in range(i + 1):
-                kM(j, i)
-
-        xT(0)
-        wkI(0)
-        wkI(1)
-        nc.vector.tensor_copy(out=emph[:], in_=emph_bf[:])
-        xC(0)
-        wkQ(0)
-        xQ(0)
-        xT(1)
-        xC(1)
-        wkQ(1)
-        xQ(1)
-        wave(0)
-        xT(2)
-        widen(2)
-        xC(2)
-        wave(1)
-        wkI(2)
-        xQ(2)
-        wkQ(2)
-        widen(2)
-        xT(3)
-        xC(3)
-        wave(2)
-        wkI(3)
-        xQ(3)
-        wkQ(3)
-        wvI(0, 0)
-        widen(2)
-        xT(4)
-        xC(4)
-        wave(3)
-        xQ(4)
-        wvQ(0, 0)
-        widen(2)
-        xT(5)
-        xC(5)
-        kA(0)
-        kA(1)
-        xQ(5)
-        for k in range(4):
-            kM(4, k)
-        wvI(0, 1)
-        kA(2)
-        kA(3)
-        widen(2)
-        xT(6)
-        xC(6)
-        for k in range(4):
-            kM(5, k)
-        xQ(6)
-        wvQ(0, 1)
-        widen(2)
-        xT(7)
-        xC(7)
-        for k in range(4):
-            kM(6, k)
-        wvI(1, 0)
-        xQ(7)
-        wvQ(1, 0)
-        kA(4)
-        kA(5)
-        for k in range(4):
-            kM(7, k)
-        widen(4)
-        kA(6)
-        wvI(2, 0)
-        kA(7)
-        wvQ(2, 0)
-        widen(4)
-        wvI(3, 0)
-        for k in range(3):
-            for i in range(8):
-                vM(i, "a", k)
-        widen(4)
-        wvI(1, 1)
-        wvQ(3, 0)
         for i in range(8):
-            vM(i, "a", 3)
-        widen(4)
-        wvI(2, 1)
-        wvQ(1, 1)
-        widen(4)
-        for i in range(4):
-            vO(i, "a")
-        wvI(3, 1)
-        wvQ(2, 1)
-        kI(0)
-        wvQ(3, 1)
-        for i in range(4, 8):
-            vO(i, "a")
-        vI(0, "a")
-        kQ(0)
-        for k in range(4):
-            for i in range(4):
-                vM(i, "b", k)
-        kI(1)
-        for i in range(4):
-            vO(i, "b")
-        vI(1, "a")
-        vQ(0, "a")
-        for i in range(4, 8):
-            for k in range(4):
-                vM(i, "b", k)
-        vQ(1, "a")
-        vI(0, "b")
-        kQ(1)
-        for i in range(4, 8):
-            vO(i, "b")
+            for q in range(2):
+                tensor_work["xT%d%d" % (i, q)] = (0, "x%d%d" % (i, q), ["x%d.load" % i], transposes(i, q))
         for i in range(4):
             for k in range(4):
-                vM(i, "c", k)
-        vQ(0, "b")
-        vI(1, "b")
-        for i in range(4):
-            vO(i, "c")
+                tensor_work["kM%d%d" % (i, k)] = (
+                    1, "k%d" % i, ["x%d" % i, "wk%d" % k],
+                    pass_of("k%d" % i, 4, 0, "x%d" % i, P * k, "wk%d" % k, 0, R),
+                )
         for i in range(4, 8):
-            for k in range(4):
-                vM(i, "c", k)
-        vQ(1, "b")
-        vI(0, "c")
-        for i in range(4, 8):
-            vO(i, "c", "SVSV"[i - 4])
-        for m in range(4):
-            for g in range(2):
-                oM(m, "a", g, m)
-        vQ(0, "c")
-        vI(1, "c")
-        for m in range(4):
-            oC(m, "a")
-        vQ(1, "c")
-        for m in range(4):
-            for g in range(2):
-                oM(m, "b", g, 4 + m)
-        for m in range(4):
-            oC(m, "b")
-        for m in range(4):
-            oM(m, "c", 0, m)
-        for m in range(4):
-            oM(m, "c", 1)
-            oC(m, "c")
+            for cb in range(4):
+                tensor_work["kN%d%d" % (i, cb)] = (
+                    1, "n1%d" % cb, ["x%d" % i] + ["wk%d" % k for k in range(4)], passes4(i, cb),
+                )
+        for b, rank in (("a", 2), ("b", 3), ("c", 5)):
+            c0, n = BLOCKS[b]
+            for i in range(8):
+                for k in range(4):
+                    w = "wv%d%d" % (k, c0 // HALF)
+                    tensor_work["vM%d%s%d" % (i, b, k)] = (
+                        rank, "v%d%s" % (i, b), ["x%d" % i, w],
+                        pass_of("v%d%s" % (i, b), 4, 0, "x%d" % i, P * k, w, c0 % HALF, n),
+                    )
+        for b, rank in (("a", 4), ("b", 6), ("c", 7)):
+            n = BLOCKS[b][1]
+            for m in range(4):
+                for g in range(2):
+                    tensor_work["oM%d%s%d" % (m, b, g)] = (
+                        rank, "o%d%s" % (m, b), ["key%d" % g, "val%d%s" % (g, b)],
+                        pass_of("o%d%s" % (m, b), 2, 0, "key%d" % g, P * m, "val%d%s" % (g, b), 0, n),
+                    )
+
+        ready = set()
+        free_banks = list(range(8))
+        state = {"tiles": 0, "transposed": 0}
+        pending = []
+
+        def announce(key):
+            ready.add(key)
+            for name, (rank, bank, needs, run) in tensor_work.items():
+                if key in needs and all(k in ready for k in needs):
+                    at = len(pending)
+                    while at > 0 and tensor_work[pending[at - 1]][0] > rank:
+                        at -= 1
+                    pending[at:at] = [name]
+
+        def flush():
+            again = True
+            while again:
+                again = False
+                for name in list(pending):
+                    rank, key, needs, run = tensor_work[name]
+                    if key not in banks:
+                        if len(free_banks) == 0:
+                            continue
+                        if rank == 0:
+                            if state["tiles"] >= 4:
+                                continue
+                            state["tiles"] += 1
+                        elif len(free_banks) <= 2 and state["transposed"] < 16:
+                            continue
+                        b = free_banks.pop(0)
+                        banks[key] = (b, psum.tile([P, 512], F32, name="bank", tag="bank%d" % b, bufs=1))
+                    if rank == 0:
+                        state["transposed"] += 1
+                    run(banks[key][1])
+                    pending.remove(name)
+                    again = True
+                    break
+
+        def release(key):
+            free_banks.append(banks[key][0])
+            banks.pop(key)
+            if key[0] == "x":
+                state["tiles"] -= 1
+
+        def row_tile(key, n):
+            if key not in rows:
+                rows[key] = work.tile(
+                    [P, PACK, n], BF16, name="rows", tag="t4" if n == 512 else "t2",
+                    bufs=32 if n == 512 else 8, align_bytes=64,
+                )
+            return rows[key]
+
+        def unit(name, engine):
+            kind, arg = name[:3], name[3:]
+            if name[:2] == "xC":
+                i, q = int(name[2]), int(name[3])
+                if q == 0 and "x%d" % i not in ils or q == 1 and "x%d" % i not in ils:
+                    il_tile("x%d" % i, 512)
+                bank = banks["x%d%d" % (i, q)][1]
+                dst = ils["x%d" % i][:, 1024 * q : 1024 * (q + 1)].bitcast(F32)
+                dst = dst.rearrange("p (g r u) -> p g r u", g=2, u=2)
+                src = bank[:].rearrange("p (g u r) -> p g r u", g=2, u=2)
+                if engine == "S":
+                    nc.scalar.copy(out=dst, in_=src)
+                else:
+                    nc.vector.tensor_copy(out=dst, in_=src)
+                release("x%d%d" % (i, q))
+            elif name[:2] == "xQ":
+                quantize("x" + name[2])
+                announce("x" + name[2])
+            elif kind == "wkI":
+                interleave("wk" + arg, raws["wk", int(arg)], engine)
+            elif kind == "wkQ":
+                quantize("wk" + arg)
+                announce("wk" + arg)
+            elif kind == "wvW":
+                g, h, p = int(arg[0]), int(arg[1]), int(arg[2])
+                wide = row_tile("w%d%d" % (g, h), 512)
+                for t in (2 * p, 2 * p + 1):
+                    scaled(
+                        wide[:, t, :], raws["wv", g][:, t, HALF * h : HALF * (h + 1)].bitcast(FP8),
+                        wv_scale[:, g, t : t + 1], engine,
+                    )
+            elif kind == "wvI":
+                interleave("wv" + arg, rows["w" + arg], engine)
+            elif kind == "wvQ":
+                quantize("wv" + arg)
+                announce("wv" + arg)
+            elif name[:2] == "kA" and len(name) == 3:
+                i = int(name[2])
+                nc.vector.tensor_tensor(
+                    out=row_tile("k%d" % (i // PACK), 512)[:, i % PACK, :], in0=banks["k%d" % i][1][:],
+                    in1=raws["pos", i // PACK][:, i % PACK, :], op=ALU.add,
+                )
+                release("k%d" % i)
+            elif name[:2] == "kA":
+                g, cb = int(name[2]), int(name[4])
+                if "sum%d" % g not in rows:
+                    rows["sum%d" % g] = work.tile([P, R * PACK], BF16, name="ksum", tag="t4", bufs=32, align_bytes=64)
+                nc.vector.tensor_tensor(
+                    out=rows["sum%d" % g][:, 512 * cb : 512 * (cb + 1)].rearrange("p (c t) -> p c t", t=PACK),
+                    in0=banks["n%d%d" % (g, cb)][1][:].rearrange("p (t c) -> p c t", t=PACK),
+                    in1=raws["pos", g][:, :, P * cb : P * (cb + 1)].rearrange("p t c -> p c t"),
+                    op=ALU.add,
+                )
+                release("n%d%d" % (g, cb))
+            elif name == "kI0":
+                interleave("key0", rows["k0"], engine, relu=True)
+            elif name == "kI1":
+                nc.vector.tensor_scalar(
+                    out=il_tile("key1", 512)[:], in0=rows["sum1"][:], scalar1=0.0, scalar2=None, op0=ALU.max
+                )
+            elif name[:2] == "kQ":
+                quantize("key" + name[2])
+                announce("key" + name[2])
+            elif name[:2] == "vO":
+                i, b = int(name[2]), name[3]
+                n = BLOCKS[b][1]
+                scaled(
+                    row_tile("v%d%s" % (i // PACK, b), n)[:, i % PACK, :], banks["v%d%s" % (i, b)][1][:, :n],
+                    emph[:, i // PACK, i % PACK : i % PACK + 1], engine,
+                )
+                release("v%d%s" % (i, b))
+            elif name[:2] == "vI":
+                interleave("val" + name[2:], rows["v" + name[2:]], engine, n=BLOCKS[name[3]][1])
+            elif name[:2] == "vQ":
+                quantize("val" + name[2:])
+                announce("val" + name[2:])
+            elif name[:2] == "oC":
+                m, b = int(name[2]), name[3]
+                c0, n = BLOCKS[b]
+                res = work.tile([P, n], F32, name="res", tag="res%d" % n, bufs=4 if n == 512 else 8)
+                bank = banks["o%d%s" % (m, b)][1]
+                if engine == "S":
+                    nc.scalar.copy(out=res[:], in_=bank[:, :n])
+                else:
+                    nc.vector.tensor_copy(out=res[:], in_=bank[:, :n])
+                release("o%d%s" % (m, b))
+                nc.sync.dma_start(out=out[P * m : P * (m + 1), c0 : c0 + n], in_=res[:])
+
+        for word in words:
+            if word[0] == "x":
+                announce(word + ".load")
+        flush()
+        for at, word in enumerate(ORDER.split()):
+            name, engine = word.split(".")
+            if at == 8:
+                nc.vector.tensor_copy(out=emph[:], in_=emph_bf[:])
+            unit(name, engine)
+            flush()

@@ -23,18 +23,19 @@ GROUPS = T // K_PASS
 HALF = 512
 BLOCKS = {"a": (0, 512), "b": (512, 256), "c": (768, 256)}
 
-LOADS = "wv0a wv0b wv2 x0 wv3 x3 x5 x4 x6 x2 wv1 x1 x7 wk3 pos0 wk2 pos1 wk1 wk0"
+WARM_UP, RUN_MAX, MM_RUN = 8, 4, 2
+LOADS = "x0a wv0a x0b wv0b x1 x2 wv1 x3 x4 wv2 x5 x6 wv3 x7 wk0 wk1 pos0 wk2 pos1 wk3"
 ORDER = """
-    wvW000.S wvW010.V wvW001.V wvI00.V wvW011.S wvW210.V wvW200.S wvW211.V wvQ00.V xC00.S wvW311.V
-    wvW301.V wvW201.S wvI20.V wvW300.S wvI30.V wvQ20.V wvQ30.V xC31.S xC30.S xC40.S xC41.S xC60.S
-    xC61.S xC20.S xQ3.V xQ4.V xQ6.V wvW100.V wvW310.V wvW101.S wvI10.V xC01.S xQ0.V xC51.S xC10.S
-    xC21.S xC70.S xC71.S xC11.S xC50.S wvW111.S wvQ10.V vO4a.S vO0a.S wkI3.V xQ2.V wvW110.S xQ1.V
-    vO1a.S xQ7.V vO7a.S wkI2.V wvI21.S vO3a.S wkQ3.V wkQ2.V wkI1.V xQ5.V wkQ1.V wkI0.V wkQ0.V kA0.V
-    kA1.V kA3.V kA2.V kA1n0.V wvI11.S wvQ11.V kA1n1.V wvQ21.V wvI01.S wvQ01.V vO6a.S wvI31.S
-    kA1n2.V vO2a.V vI0a.S kA1n3.V vO5a.V wvQ31.V vO1b.S vO0b.S vO7b.S vO3b.S vO4b.S vO6b.S vO2b.S
-    vO5b.S vO0c.S vO1c.S vI1b.S vO3c.S vO5c.S vO6c.S vO4c.S vI1a.V vQ1a.V vQ0a.V vO7c.S kI1.V kQ1.V
-    kI0.V kQ0.V oC0a.S oC3a.S oC2a.S vO2c.V vI0c.V vI0b.V vQ0b.V oC1a.V vQ1b.V oC0b.S oC3b.S oC1b.S
-    oC2b.S vQ0c.V vI1c.V vQ1c.V oC0c.V oC1c.S oC3c.V oC2c.V
+    wvW001.V wvW000.S xC00.S wvW011.V xC01.S wvI00.V wvW010.S xQ0.V wvW100.S wvQ00.V xC10.S
+    wvW101.V xC11.S wvI10.V xC20.S wvW111.V xC21.S xQ1.V wvW110.S wvQ10.V wvW200.S xQ2.V xC30.S
+    wvW201.V xC31.S wvI20.V xC40.S wvW211.V xC41.S xQ3.V wvW210.S wvQ20.V wvW300.S xQ4.V xC50.S
+    wvW301.V xC51.S wvI30.V xC60.S wvW311.V xC61.S xQ5.V wvW310.S wvQ30.V xC70.S xQ6.V xC71.S
+    wkI0.V wkI3.S xQ7.V vO0a.S wkQ0.V vO1a.S wkI1.V vO2a.S wkI2.V vO3a.S wkQ1.V vO4a.S wkQ2.V
+    wvI11.S wkQ3.V vO5a.S vO6a.S kA0.V wvI21.S kA1.V vO7a.S kA2.V wvI31.S kA3.V vI0a.S wvI01.V
+    wvQ01.V wvQ11.V kA1n0.V kA1n1.V wvQ21.V kA1n2.V kA1n3.V wvQ31.V vO0b.S vO1b.S vO2b.S vO3b.S
+    vO4b.S vO5b.S vO6b.S vO7b.S vO0c.S kI0.V vO1c.S kI1.V vI0b.S kQ1.V vO2c.S vI1a.V vO3c.S vQ0a.V
+    vO4c.S kQ0.V vO5c.S vQ1a.V vO6c.S vI1b.V vO7c.S vQ1b.V oC0a.S vQ0b.V oC2a.S vI0c.V oC1a.S
+    vQ0c.V oC0b.S oC3a.V oC1b.S vI1c.V oC2b.S vQ1c.V oC3b.S oC0c.V oC1c.S oC3c.V oC2c.S
 """
 
 
@@ -68,13 +69,16 @@ def tile_text_image_memory_bridge_s7_kernel(
         def load(word):
             stem = word[:-1] if word[-1] in "ab" else word
             kind, n = stem[:-1], int(stem[-1])
-            if word[-1] == "a":
-                nc.sync.dma_start(out=raw_tile(kind, n)[:, 0:2, :], in_=wv_v[n][:, 0:2, :])
-            elif word[-1] == "b":
-                nc.sync.dma_start(out=raws[kind, n][:, 2:4, :], in_=wv_v[n][:, 2:4, :])
+            if (kind, n) not in raws:
+                raw_tile(kind, n)
+            tile = raws[kind, n]
+            view = x_v[n // PACK, n % PACK] if kind == "x" else {"wk": wk_v, "wv": wv_v, "pos": pos_v}[kind][n]
+            if word[-1] in "ab":
+                half = "ab".index(word[-1])
+                cut = slice(half * D // 2, (half + 1) * D // 2) if kind == "x" else slice(2 * half, 2 * half + 2)
+                nc.sync.dma_start(out=tile[:, cut], in_=view[:, cut])
             else:
-                view = x_v[n // PACK, n % PACK] if kind == "x" else {"wk": wk_v, "wv": wv_v, "pos": pos_v}[kind][n]
-                nc.sync.dma_start(out=raw_tile(kind, n)[:], in_=view)
+                nc.sync.dma_start(out=tile[:], in_=view)
 
         words = LOADS.split()
         load(words[0])
@@ -87,6 +91,8 @@ def tile_text_image_memory_bridge_s7_kernel(
         nc.scalar.dma_start(out=emph_bf[:], in_=emphasis.rearrange("(g p t) -> p g t", p=P, t=PACK))
         for word in words[2:]:
             load(word)
+        zeros = keep.tile([P, P + 512], BF16, name="zeros")
+        nc.gpsimd.memset(zeros[:], 0.0)
         ident = keep.tile([P, P], F32, name="ident")
         make_identity(nc, ident[:])
         emph = keep.tile([P, GROUPS, PACK], F32, name="emph")
@@ -167,7 +173,7 @@ def tile_text_image_memory_bridge_s7_kernel(
 
         for i in range(8):
             for q in range(2):
-                tensor_work["xT%d%d" % (i, q)] = (0, "x%d%d" % (i, q), ["x%d.load" % i], transposes(i, q))
+                tensor_work["xT%d%d" % (i, q)] = (0, "x%d%d" % (i, q), ["x%d.load" % i if i else "x0%s.load" % "ab"[q]], transposes(i, q))
         for i in range(4):
             for k in range(4):
                 tensor_work["kM%d%d" % (i, k)] = (
@@ -199,7 +205,7 @@ def tile_text_image_memory_bridge_s7_kernel(
 
         ready = set()
         free_banks = list(range(8))
-        state = {"tiles": 0, "transposed": 0}
+        state = {"tiles": 0, "transposed": 0, "run": 0, "matmuls": 0}
         pending = []
 
         def announce(key):
@@ -211,29 +217,45 @@ def tile_text_image_memory_bridge_s7_kernel(
                         at -= 1
                     pending[at:at] = [name]
 
+        def warm(bank):
+            nc.tensor.matmul(bank[:], zeros[:, :P], zeros[:, P:], start=True, stop=True)
+
+        def take(matmuls_only):
+            for name in list(pending):
+                rank, key, needs, run = tensor_work[name]
+                if rank == 0 and matmuls_only:
+                    continue
+                if key not in banks:
+                    if len(free_banks) == 0:
+                        continue
+                    if rank == 0:
+                        if state["tiles"] >= 4:
+                            continue
+                        state["tiles"] += 1
+                    elif len(free_banks) <= 2 and state["transposed"] < 16:
+                        continue
+                    b = free_banks.pop(0)
+                    banks[key] = (b, psum.tile([P, 512], F32, name="bank", tag="bank%d" % b, bufs=1))
+                if rank == 0:
+                    for turn in range(WARM_UP if state["transposed"] == 0 else int(state["run"] >= RUN_MAX)):
+                        warm(banks[key][1])
+                        state["run"] = 0
+                    state["transposed"] += 1
+                    state["run"] += 4
+                    state["matmuls"] = 0
+                else:
+                    state["run"] = 0
+                    state["matmuls"] += 1
+                run(banks[key][1])
+                pending.remove(name)
+                return True
+            return False
+
         def flush():
             again = True
             while again:
-                again = False
-                for name in list(pending):
-                    rank, key, needs, run = tensor_work[name]
-                    if key not in banks:
-                        if len(free_banks) == 0:
-                            continue
-                        if rank == 0:
-                            if state["tiles"] >= 4:
-                                continue
-                            state["tiles"] += 1
-                        elif len(free_banks) <= 2 and state["transposed"] < 16:
-                            continue
-                        b = free_banks.pop(0)
-                        banks[key] = (b, psum.tile([P, 512], F32, name="bank", tag="bank%d" % b, bufs=1))
-                    if rank == 0:
-                        state["transposed"] += 1
-                    run(banks[key][1])
-                    pending.remove(name)
-                    again = True
-                    break
+                first = state["run"] >= RUN_MAX or (state["run"] == 0 and state["matmuls"] < MM_RUN)
+                again = (first and take(True)) or take(False)
 
         def release(key):
             free_banks.append(banks[key][0])

@@ -21,21 +21,21 @@ K_PASS = P * PACK
 D_PASSES = D // K_PASS
 GROUPS = T // K_PASS
 HALF = 512
+T4 = 22
 BLOCKS = {"a": (0, 512), "b": (512, 256), "c": (768, 256)}
 
-WARM_UP, RUN_MAX, MM_RUN = 8, 4, 2
-LOADS = "x0a wv0a x0b wv0b x1 x2 wv1 x3 x4 wv2 x5 x6 wv3 x7 wk0 wk1 pos0 wk2 pos1 wk3"
+WARM_UP, RUN_MAX, MM_RUN = 0, 999, 0
+LOADS = "wv0a wv2 wv3 x0a x2 x3 wv0b x0b x6 x7 x4 x1 x5 wv1 pos1 wk3 wk0 wk2 wk1 pos0"
 ORDER = """
-    wvW001.V wvW000.S xC00.S wvW011.V xC01.S wvI00.V wvW010.S xQ0.V wvW100.S wvQ00.V xC10.S
-    wvW101.V xC11.S wvI10.V xC20.S wvW111.V xC21.S xQ1.V wvW110.S wvQ10.V wvW200.S xQ2.V xC30.S
-    wvW201.V xC31.S wvI20.V xC40.S wvW211.V xC41.S xQ3.V wvW210.S wvQ20.V wvW300.S xQ4.V xC50.S
-    wvW301.V xC51.S wvI30.V xC60.S wvW311.V xC61.S xQ5.V wvW310.S wvQ30.V xC70.S xQ6.V xC71.S
-    wkI0.V wkI3.S xQ7.V vO0a.S wkQ0.V vO1a.S wkI1.V vO2a.S wkI2.V vO3a.S wkQ1.V vO4a.S wkQ2.V
-    wvI11.S wkQ3.V vO5a.S vO6a.S kA0.V wvI21.S kA1.V vO7a.S kA2.V wvI31.S kA3.V vI0a.S wvI01.V
-    wvQ01.V wvQ11.V kA1n0.V kA1n1.V wvQ21.V kA1n2.V kA1n3.V wvQ31.V vO0b.S vO1b.S vO2b.S vO3b.S
-    vO4b.S vO5b.S vO6b.S vO7b.S vO0c.S kI0.V vO1c.S kI1.V vI0b.S kQ1.V vO2c.S vI1a.V vO3c.S vQ0a.V
-    vO4c.S kQ0.V vO5c.S vQ1a.V vO6c.S vI1b.V vO7c.S vQ1b.V oC0a.S vQ0b.V oC2a.S vI0c.V oC1a.S
-    vQ0c.V oC0b.S oC3a.V oC1b.S vI1c.V oC2b.S vQ1c.V oC3b.S oC0c.V oC1c.S oC3c.V oC2c.S
+    wvW20.S wvW00.V wvW21.V wvW30.V wvI20.V xC00.V wvQ20.V wvW31.S wvI31.V wvI30.V wvW01.S wvI00.V
+    wvQ30.V wvQ00.V xC30.S xC01.S xC60.S xC61.S xC70.S xC71.S xC40.S xC41.S xC10.S xC11.S xC50.S
+    xQ6.V xQ0.V xQ7.V xQ4.V wvW10.V wvW11.V xQ1.V xC21.S xC51.S xQ5.V xC31.S xQ3.V xC20.S xQ2.V
+    wkI2.V wvI10.S wvQ10.V wkI1.V wkQ2.V wkI3.S wkQ3.V vO1a.S vO3a.S wkQ1.V wkI0.V vO5a.S vO6a.S
+    vO0a.V wvI21.S wkQ0.V kA0.V kA2.V kA3.V wvI11.V wvQ11.V vO2a.S vI0a.S vQ0a.V wvQ21.V vO7a.S
+    wvQ31.V wvI01.S kA1n3.V kA1.V kA1n0.V vO4a.S vI1a.S wvQ01.V vO0d.S vO2d.S vO1d.S vO3d.S vO5d.S
+    vO4d.S vO7d.S kA1n2.V kI0.V kQ0.V kA1n1.V vQ1a.V kI1.V kQ1.V oC0a.S oC1a.S oC3a.S oC2a.S vI0c.V
+    vI0b.V vO6d.V vI1b.V vQ0b.V vQ1b.V oC0b.S oC2b.S vQ0c.V vI1c.V vQ1c.V oC1c.S oC0c.V oC3c.V
+    oC2c.S
 """
 
 
@@ -63,7 +63,8 @@ def tile_text_image_memory_bridge_s7_kernel(
                 "wv": ([P, PACK, C], U8),
                 "pos": ([P, PACK, R], BF16),
             }[kind]
-            raws[kind, n] = work.tile(shape, dtype, name=kind + "raw", tag="pos" if kind == "pos" else "t4", bufs=2 if kind == "pos" else 32, align_bytes=64)
+            raws[kind, n] = work.tile(shape, dtype, name=kind + "raw", tag=kind if kind in ("pos", "wv") else "t4",
+                bufs={"pos": 2, "wv": 4}.get(kind, T4), align_bytes=64)
             return raws[kind, n]
 
         def load(word):
@@ -81,15 +82,16 @@ def tile_text_image_memory_bridge_s7_kernel(
                 nc.sync.dma_start(out=tile[:], in_=view)
 
         words = LOADS.split()
-        load(words[0])
-        load(words[1])
         wv_scale = keep.tile([P, D_PASSES, PACK], F32, name="wvscale")
         nc.scalar.dma_start(
             out=wv_scale[:], in_=w_value_scale.rearrange("(g p t) o -> p g (t o)", p=P, t=PACK)
         )
         emph_bf = keep.tile([P, GROUPS, PACK], BF16, name="emphbf")
         nc.scalar.dma_start(out=emph_bf[:], in_=emphasis.rearrange("(g p t) -> p g t", p=P, t=PACK))
-        for word in words[2:]:
+        first = keep.tile([P, 1], F32, name="first")
+        nc.vector.memset(first[:], 0.0)
+        nc.scalar.activation(out=first[:], in_=first[:], func=COPY)
+        for word in words:
             load(word)
         zeros = keep.tile([P, P + 512], BF16, name="zeros")
         nc.gpsimd.memset(zeros[:], 0.0)
@@ -110,14 +112,16 @@ def tile_text_image_memory_bridge_s7_kernel(
         def il_tile(key, n):
             ils[key] = work.tile(
                 [P, n * PACK], BF16, name="il", tag="t4" if n == 512 else "t2",
-                bufs=32 if n == 512 else 8, align_bytes=64
+                bufs=T4 if n == 512 else 4, align_bytes=64
             )
             return ils[key]
 
         def interleave(key, src, engine, n=512, relu=False):
             dst = il_tile(key, n)[:].rearrange("p (c i t) -> p c t i", i=4, t=PACK)
-            src = src[:].rearrange("p t (c i) -> p c t i", i=4)
-            if relu:
+            src = src.rearrange("p t (c i) -> p c t i", i=4)
+            if relu and engine == "S":
+                nc.scalar.activation(out=dst, in_=src, func=mybir.ActivationFunctionType.Relu)
+            elif relu:
                 nc.vector.tensor_scalar(out=dst, in0=src, scalar1=0.0, scalar2=None, op0=ALU.max)
             elif engine == "S":
                 nc.scalar.copy(out=dst, in_=src)
@@ -185,22 +189,26 @@ def tile_text_image_memory_bridge_s7_kernel(
                 tensor_work["kN%d%d" % (i, cb)] = (
                     1, "n1%d" % cb, ["x%d" % i] + ["wk%d" % k for k in range(4)], passes4(i, cb),
                 )
-        for b, rank in (("a", 2), ("b", 3), ("c", 5)):
-            c0, n = BLOCKS[b]
+        for h in range(2):
             for i in range(8):
                 for k in range(4):
-                    w = "wv%d%d" % (k, c0 // HALF)
+                    w = "wv%d%d" % (k, h)
+                    b = "ad"[h]
                     tensor_work["vM%d%s%d" % (i, b, k)] = (
-                        rank, "v%d%s" % (i, b), ["x%d" % i, w],
-                        pass_of("v%d%s" % (i, b), 4, 0, "x%d" % i, P * k, w, c0 % HALF, n),
+                        2 + h, "v%d%s" % (i, b), ["x%d" % i, w],
+                        pass_of("v%d%s" % (i, b), 4, 0, "x%d" % i, P * k, w, 0, HALF),
                     )
         for b, rank in (("a", 4), ("b", 6), ("c", 7)):
             n = BLOCKS[b][1]
             for m in range(4):
                 for g in range(2):
+                    pair = m % 2 if b == "b" else 0
+                    needs = ["key%d" % g, "val%d%s" % (g, b)]
+                    if pair:
+                        needs += ["oM%db0" % (m - 1), "oM%db1" % (m - 1)]
                     tensor_work["oM%d%s%d" % (m, b, g)] = (
-                        rank, "o%d%s" % (m, b), ["key%d" % g, "val%d%s" % (g, b)],
-                        pass_of("o%d%s" % (m, b), 2, 0, "key%d" % g, P * m, "val%d%s" % (g, b), 0, n),
+                        rank, "o%d%s" % (m - pair, b), needs,
+                        pass_of("o%d%s" % (m, b), 2, n * pair, "key%d" % g, P * m, "val%d%s" % (g, b), 0, n),
                     )
 
         ready = set()
@@ -248,6 +256,7 @@ def tile_text_image_memory_bridge_s7_kernel(
                     state["matmuls"] += 1
                 run(banks[key][1])
                 pending.remove(name)
+                announce(name)
                 return True
             return False
 
@@ -267,7 +276,7 @@ def tile_text_image_memory_bridge_s7_kernel(
             if key not in rows:
                 rows[key] = work.tile(
                     [P, PACK, n], BF16, name="rows", tag="t4" if n == 512 else "t2",
-                    bufs=32 if n == 512 else 8, align_bytes=64,
+                    bufs=T4 if n == 512 else 4, align_bytes=64,
                 )
             return rows[key]
 
@@ -290,20 +299,22 @@ def tile_text_image_memory_bridge_s7_kernel(
                 quantize("x" + name[2])
                 announce("x" + name[2])
             elif kind == "wkI":
-                interleave("wk" + arg, raws["wk", int(arg)], engine)
+                interleave("wk" + arg, raws["wk", int(arg)][:], engine)
             elif kind == "wkQ":
                 quantize("wk" + arg)
                 announce("wk" + arg)
             elif kind == "wvW":
-                g, h, p = int(arg[0]), int(arg[1]), int(arg[2])
-                wide = row_tile("w%d%d" % (g, h), 512)
+                g, p = int(arg[0]), int(arg[1])
+                if "w%d" % g not in rows:
+                    rows["w%d" % g] = work.tile([P, PACK, C], BF16, name="wide", tag="wide", bufs=4, align_bytes=64)
                 for t in (2 * p, 2 * p + 1):
                     scaled(
-                        wide[:, t, :], raws["wv", g][:, t, HALF * h : HALF * (h + 1)].bitcast(FP8),
+                        rows["w%d" % g][:, t, :], raws["wv", g][:, t, :].bitcast(FP8),
                         wv_scale[:, g, t : t + 1], engine,
                     )
             elif kind == "wvI":
-                interleave("wv" + arg, rows["w" + arg], engine)
+                h = int(arg[1])
+                interleave("wv" + arg, rows["w" + arg[0]][:, :, HALF * h : HALF * (h + 1)], engine)
             elif kind == "wvQ":
                 quantize("wv" + arg)
                 announce("wv" + arg)
@@ -317,7 +328,7 @@ def tile_text_image_memory_bridge_s7_kernel(
             elif name[:2] == "kA":
                 g, cb = int(name[2]), int(name[4])
                 if "sum%d" % g not in rows:
-                    rows["sum%d" % g] = work.tile([P, R * PACK], BF16, name="ksum", tag="t4", bufs=32, align_bytes=64)
+                    rows["sum%d" % g] = work.tile([P, R * PACK], BF16, name="ksum", tag="t4", bufs=T4, align_bytes=64)
                 nc.vector.tensor_tensor(
                     out=rows["sum%d" % g][:, 512 * cb : 512 * (cb + 1)].rearrange("p (c t) -> p c t", t=PACK),
                     in0=banks["n%d%d" % (g, cb)][1][:].rearrange("p (t c) -> p c t", t=PACK),
@@ -326,7 +337,7 @@ def tile_text_image_memory_bridge_s7_kernel(
                 )
                 release("n%d%d" % (g, cb))
             elif name == "kI0":
-                interleave("key0", rows["k0"], engine, relu=True)
+                interleave("key0", rows["k0"][:], engine, relu=True)
             elif name == "kI1":
                 nc.vector.tensor_scalar(
                     out=il_tile("key1", 512)[:], in0=rows["sum1"][:], scalar1=0.0, scalar2=None, op0=ALU.max
@@ -336,28 +347,35 @@ def tile_text_image_memory_bridge_s7_kernel(
                 announce("key" + name[2])
             elif name[:2] == "vO":
                 i, b = int(name[2]), name[3]
-                n = BLOCKS[b][1]
                 scaled(
-                    row_tile("v%d%s" % (i // PACK, b), n)[:, i % PACK, :], banks["v%d%s" % (i, b)][1][:, :n],
+                    row_tile("v%d%s" % (i // PACK, b), HALF)[:, i % PACK, :], banks["v%d%s" % (i, b)][1][:],
                     emph[:, i // PACK, i % PACK : i % PACK + 1], engine,
                 )
                 release("v%d%s" % (i, b))
             elif name[:2] == "vI":
-                interleave("val" + name[2:], rows["v" + name[2:]], engine, n=BLOCKS[name[3]][1])
+                g, b = name[2], name[3]
+                src = rows["v" + g + ("a" if b == "a" else "d")]
+                cut = slice(0, HALF) if b == "a" else slice(BLOCKS[b][0] - HALF, BLOCKS[b][0] - HALF + BLOCKS[b][1])
+                interleave("val" + name[2:], src[:, :, cut], engine, n=BLOCKS[b][1])
             elif name[:2] == "vQ":
                 quantize("val" + name[2:])
                 announce("val" + name[2:])
             elif name[:2] == "oC":
                 m, b = int(name[2]), name[3]
                 c0, n = BLOCKS[b]
-                res = work.tile([P, n], F32, name="res", tag="res%d" % n, bufs=4 if n == 512 else 8)
+                rows_m = 2 if b == "b" else 1
+                w = n * rows_m
+                res = work.tile([P, w], F32, name="res", tag="res%d" % w, bufs=6 if w == 512 else 4)
                 bank = banks["o%d%s" % (m, b)][1]
                 if engine == "S":
-                    nc.scalar.copy(out=res[:], in_=bank[:, :n])
+                    nc.scalar.copy(out=res[:], in_=bank[:, :w])
                 else:
-                    nc.vector.tensor_copy(out=res[:], in_=bank[:, :n])
+                    nc.vector.tensor_copy(out=res[:], in_=bank[:, :w])
                 release("o%d%s" % (m, b))
-                nc.sync.dma_start(out=out[P * m : P * (m + 1), c0 : c0 + n], in_=res[:])
+                nc.sync.dma_start(
+                    out=out[P * m : P * (m + rows_m), c0 : c0 + n].rearrange("(m p) c -> p m c", p=P),
+                    in_=res[:].rearrange("p (m c) -> p m c", c=n),
+                )
 
         for word in words:
             if word[0] == "x":

@@ -8,34 +8,49 @@ FLOPS = 2 * T * D * (R + C) + 2 * T * R * C
 
 F32 = mybir.dt.float32
 BF16 = mybir.dt.bfloat16
-U32 = mybir.dt.uint32
 U8 = mybir.dt.uint8
 FP8 = mybir.dt.float8_e4m3fn
 FP8X4 = mybir.dt.float8_e4m3fn_x4
-ALU = mybir.AluOpType
+ADD = mybir.AluOpType.add
+MAX = mybir.AluOpType.max
+MULT = mybir.AluOpType.mult
 COPY = mybir.ActivationFunctionType.Copy
+RELU = mybir.ActivationFunctionType.Relu
 
 P = 128
 PACK = 4
-K_PASS = P * PACK
-D_PASSES = D // K_PASS
-GROUPS = T // K_PASS
-HALF = 512
-T4 = 22
+PASS = P * PACK
+D_PASSES = D // PASS
+GROUPS = T // PASS
+X_TILES = T // P
+M_TILES = R // P
+BANK = 512
+BANKS = 8
+
 BLOCKS = {"a": (0, 512), "b": (512, 256), "c": (768, 256)}
 
-WARM_UP, RUN_MAX, MM_RUN = 0, 999, 0
-LOADS = "wv0a wv2 wv3 x0a x2 x3 wv0b x0b x6 x7 x4 x1 x5 wv1 pos1 wk3 wk0 wk2 wk1 pos0"
+SLOTS = 22
+
+LOADS = "wv0a wv2 wv3 x0a wv0b x0b x3 x6 x1 x7 x4 x2 x5 wv1 pos1 wk3 wk2 wk0 wk1 pos0"
+
 ORDER = """
-    wvW20.S wvW00.V wvW21.V wvW30.V wvI20.V xC00.V wvQ20.V wvW31.S wvI31.V wvI30.V wvW01.S wvI00.V
-    wvQ30.V wvQ00.V xC30.S xC01.S xC60.S xC61.S xC70.S xC71.S xC40.S xC41.S xC10.S xC11.S xC50.S
-    xQ6.V xQ0.V xQ7.V xQ4.V wvW10.V wvW11.V xQ1.V xC21.S xC51.S xQ5.V xC31.S xQ3.V xC20.S xQ2.V
-    wkI2.V wvI10.S wvQ10.V wkI1.V wkQ2.V wkI3.S wkQ3.V vO1a.S vO3a.S wkQ1.V wkI0.V vO5a.S vO6a.S
-    vO0a.V wvI21.S wkQ0.V kA0.V kA2.V kA3.V wvI11.V wvQ11.V vO2a.S vI0a.S vQ0a.V wvQ21.V vO7a.S
-    wvQ31.V wvI01.S kA1n3.V kA1.V kA1n0.V vO4a.S vI1a.S wvQ01.V vO0d.S vO2d.S vO1d.S vO3d.S vO5d.S
-    vO4d.S vO7d.S kA1n2.V kI0.V kQ0.V kA1n1.V vQ1a.V kI1.V kQ1.V oC0a.S oC1a.S oC3a.S oC2a.S vI0c.V
-    vI0b.V vO6d.V vI1b.V vQ0b.V vQ1b.V oC0b.S oC2b.S vQ0c.V vI1c.V vQ1c.V oC1c.S oC0c.V oC3c.V
-    oC2c.S
+    factors@V widen.0.0@V widen.2.1@V widen.3.0@V widen.2.0@S interleave.wv20@V widen.3.1@S
+    words.0.0@V widen.0.1@S quantize.wv20@V words.3.0@S words.0.1@S words.6.0@S words.6.1@S
+    interleave.wv31@V interleave.wv30@V interleave.wv00@V words.7.0@S words.7.1@S words.4.0@S
+    words.4.1@S words.2.0@S words.1.1@S words.1.0@S quantize.x0@V quantize.wv30@V words.3.1@S
+    quantize.wv00@V quantize.x6@V quantize.x7@V words.5.1@S quantize.x4@V widen.1.1@V widen.1.0@V
+    quantize.x1@V words.5.0@S words.2.1@S quantize.x5@V interleave.wv10@S interleave.wk3@S
+    quantize.x2@V quantize.x3@V interleave.wk2@V quantize.wv10@V interleave.wk1@V emphasis.1.0@S
+    quantize.wk2@V quantize.wk3@V emphasis.2.0@S quantize.wk1@V quantize.wv31@V emphasis.3.0@S
+    emphasis.4.0@S emphasis.5.0@S emphasis.0.0@V interleave.wk0@V quantize.wk0@V interleave.wv01@S
+    emphasis.6.0@S emphasis.7.0@V pos.1@V quantize.wv01@V interleave.wv21@S pos.0@V pos.3@V
+    quantize.wv21@V interleave.wv11@V pos.2@V interleave.val0a@V quantize.wv11@V quantize.val0a@V
+    pos.1.2@V interleave.key0@S pos.1.0@V interleave.val1a@S pos.1.3@V quantize.key0@V
+    quantize.val1a@V pos.1.1@V emphasis.2.1@V emphasis.5.1@S interleave.key1@V quantize.key1@V
+    emphasis.1.1@V emphasis.0.1@S emphasis.6.1@S emphasis.3.1@S emphasis.4.1@V emphasis.7.1@S
+    interleave.val0b@V interleave.val1b@V store.0.a@S quantize.val0b@V store.1.a@S store.2.a@S
+    quantize.val1b@V store.3.a@S interleave.val1c@V interleave.val0c@V quantize.val1c@V
+    store.0.b@S quantize.val0c@V store.2.b@V store.0.c@V store.1.c@S store.2.c@S store.3.c@V
 """
 
 
@@ -44,346 +59,344 @@ def tile_text_image_memory_bridge_s7_kernel(
 ):
     nc = tc.nc
     with ExitStack() as ctx:
-        work = ctx.enter_context(tc.tile_pool(name="work", bufs=4))
+        work = ctx.enter_context(tc.tile_pool(name="work", bufs=1))
         keep = ctx.enter_context(tc.tile_pool(name="keep", bufs=1))
         psum = ctx.enter_context(tc.psum_pool(name="psum", bufs=1))
         ctx.enter_context(tc.manual_schedule())
 
-        x_v = x.rearrange("(g m t) k -> g t m k", g=GROUPS, t=PACK)
-        wk_v = w_key.rearrange("(g p t) n -> g p t n", p=P, t=PACK)
-        wv_v = w_value_bytes.rearrange("(g p t) n -> g p t n", p=P, t=PACK)
-        pos_v = pos.rearrange("(g p t) n -> g p t n", p=P, t=PACK)
+        def slot(shape):
+            return work.tile(shape, BF16, name="slot", tag="slot", bufs=SLOTS, align_bytes=64)
 
-        raws = {}
+        views = {
+            "x": x.rearrange("(g p t) k -> g t p k", p=P, t=PACK),
+            "wk": w_key.rearrange("(g p t) n -> g p t n", p=P, t=PACK),
+            "wv": w_value_bytes.rearrange("(g p t) n -> g p t n", p=P, t=PACK),
+            "pos": pos.rearrange("(g p t) n -> g p t n", p=P, t=PACK),
+        }
+        raw = {}
 
-        def raw_tile(kind, n):
-            shape, dtype = {
-                "x": ([P, D], BF16),
-                "wk": ([P, PACK, R], BF16),
-                "wv": ([P, PACK, C], U8),
-                "pos": ([P, PACK, R], BF16),
-            }[kind]
-            raws[kind, n] = work.tile(shape, dtype, name=kind + "raw", tag=kind if kind in ("pos", "wv") else "t4",
-                bufs={"pos": 2, "wv": 4}.get(kind, T4), align_bytes=64)
-            return raws[kind, n]
+        def raw_tile(kind):
+            if kind == "x":
+                return slot([P, D])
+            if kind == "wk":
+                return slot([P, PACK, R])
+            if kind == "wv":
+                return work.tile([P, PACK, C], U8, name="bytes", tag="bytes", bufs=D_PASSES, align_bytes=64)
+            return work.tile([P, PACK, R], BF16, name="pos", tag="pos", bufs=GROUPS, align_bytes=64)
 
         def load(word):
-            stem = word[:-1] if word[-1] in "ab" else word
-            kind, n = stem[:-1], int(stem[-1])
-            if (kind, n) not in raws:
-                raw_tile(kind, n)
-            tile = raws[kind, n]
-            view = x_v[n // PACK, n % PACK] if kind == "x" else {"wk": wk_v, "wv": wv_v, "pos": pos_v}[kind][n]
-            if word[-1] in "ab":
-                half = "ab".index(word[-1])
-                cut = slice(half * D // 2, (half + 1) * D // 2) if kind == "x" else slice(2 * half, 2 * half + 2)
-                nc.sync.dma_start(out=tile[:, cut], in_=view[:, cut])
-            else:
-                nc.sync.dma_start(out=tile[:], in_=view)
+            half = word[-1] if word[-1] in "ab" else ""
+            key = word[:-1] if half else word
+            kind, n = key[:-1], int(key[-1])
+            if key not in raw:
+                raw[key] = raw_tile(kind)
+            source = views["x"][n // PACK, n % PACK] if kind == "x" else views[kind][n]
+            extent = D if kind == "x" else PACK
+            cut = slice(0, extent)
+            if half == "a":
+                cut = slice(0, extent // 2)
+            elif half == "b":
+                cut = slice(extent // 2, extent)
+            nc.sync.dma_start(out=raw[key][:, cut], in_=source[:, cut])
 
-        words = LOADS.split()
-        wv_scale = keep.tile([P, D_PASSES, PACK], F32, name="wvscale")
+        wv_scale = keep.tile([P, D_PASSES, PACK], F32, name="wv_scale")
         nc.scalar.dma_start(
             out=wv_scale[:], in_=w_value_scale.rearrange("(g p t) o -> p g (t o)", p=P, t=PACK)
         )
-        emph_bf = keep.tile([P, GROUPS, PACK], BF16, name="emphbf")
-        nc.scalar.dma_start(out=emph_bf[:], in_=emphasis.rearrange("(g p t) -> p g t", p=P, t=PACK))
-        first = keep.tile([P, 1], F32, name="first")
-        nc.vector.memset(first[:], 0.0)
-        nc.scalar.activation(out=first[:], in_=first[:], func=COPY)
-        for word in words:
+        emphasis_bf = keep.tile([P, GROUPS, PACK], BF16, name="emphasis_bf")
+        nc.scalar.dma_start(out=emphasis_bf[:], in_=emphasis.rearrange("(g p t) -> p g t", p=P, t=PACK))
+        table = keep.tile([P, 1], F32, name="table")
+        nc.vector.memset(table[:], 0.0)
+        nc.scalar.activation(out=table[:], in_=table[:], func=COPY)
+        for word in LOADS.split():
             load(word)
-        zeros = keep.tile([P, P + 512], BF16, name="zeros")
-        nc.gpsimd.memset(zeros[:], 0.0)
-        ident = keep.tile([P, P], F32, name="ident")
-        make_identity(nc, ident[:])
-        emph = keep.tile([P, GROUPS, PACK], F32, name="emph")
+        identity = keep.tile([P, P], F32, name="identity")
+        make_identity(nc, identity[:])
+        emphasis_f32 = keep.tile([P, GROUPS, PACK], F32, name="emphasis_f32")
 
-        codes, scales, ils, rows, banks = {}, {}, {}, {}, {}
+        s_words = X_TILES * PASS + GROUPS * R
+        m_words = D_PASSES * (R + C) + GROUPS * C
+        store = {}
+        for kind, each, words, start in (
+            ("stationary", PACK, s_words, 0),
+            ("moving", PACK, m_words, 64),
+            ("stationary", 1, s_words, 128),
+            ("moving", 1, m_words, 192),
+        ):
+            tile = keep.tile([P, 256 + each * words], U8, name="store_%s%d" % (kind, each), align_bytes=256)
+            store[kind, each] = (tile, [start])
+
+        def store_bytes(kind, each, words):
+            tile, ends = store[kind, each]
+            ends.append(ends[-1] + each * words)
+            return tile[:, ends[-2] : ends[-1]]
+
+        source, codes, scales = {}, {}, {}
 
         def quantize(key):
-            src = ils[key][:]
-            width = src.shape[1] // PACK
-            c = keep.tile([P, width], U32, name="c_" + key, align_bytes=64)
-            s = keep.tile([P, width], U8, name="s_" + key, align_bytes=64)
-            nc.vector.quantize_mx(out=c[:].bitcast(FP8X4), scales=s[:], in_=src)
-            codes[key], scales[key] = c, s
+            values = source[key][:]
+            words = values.shape[1] // PACK
+            kind = "stationary" if key[0] in "xk" else "moving"
+            codes[key] = store_bytes(kind, PACK, words)
+            scales[key] = store_bytes(kind, 1, words)
+            nc.vector.quantize_mx(out=codes[key].bitcast(FP8X4), scales=scales[key], in_=values)
 
-        def il_tile(key, n):
-            ils[key] = work.tile(
-                [P, n * PACK], BF16, name="il", tag="t4" if n == 512 else "t2",
-                bufs=T4 if n == 512 else 4, align_bytes=64
-            )
-            return ils[key]
-
-        def interleave(key, src, engine, n=512, relu=False):
-            dst = il_tile(key, n)[:].rearrange("p (c i t) -> p c t i", i=4, t=PACK)
-            src = src.rearrange("p t (c i) -> p c t i", i=4)
-            if relu and engine == "S":
-                nc.scalar.activation(out=dst, in_=src, func=mybir.ActivationFunctionType.Relu)
-            elif relu:
-                nc.vector.tensor_scalar(out=dst, in0=src, scalar1=0.0, scalar2=None, op0=ALU.max)
-            elif engine == "S":
-                nc.scalar.copy(out=dst, in_=src)
-            else:
-                nc.vector.tensor_copy(out=dst, in_=src)
-
-        def scaled(dst, src, scale, engine):
-            if engine == "S":
-                nc.scalar.activation(out=dst, in_=src, func=COPY, scale=scale)
-            else:
-                nc.vector.tensor_scalar(out=dst, in0=src, scalar1=scale, scalar2=None, op0=ALU.mult)
-
-        def mm(bank, lhs, lcol, rhs, rcol, n, start, stop):
+        def multiply(bank, lhs, lhs_col, rhs, rhs_col, n, start, stop):
             nc.tensor.matmul_mx(
                 out=bank,
-                lhsT=codes[lhs][:, lcol : lcol + P].bitcast(FP8X4),
-                lhsT_scale=scales[lhs][:, lcol : lcol + P],
-                rhs=codes[rhs][:, rcol : rcol + n].bitcast(FP8X4),
-                rhs_scale=scales[rhs][:, rcol : rcol + n],
+                lhsT=codes[lhs][:, PACK * lhs_col : PACK * (lhs_col + P)].bitcast(FP8X4),
+                lhsT_scale=scales[lhs][:, lhs_col : lhs_col + P],
+                rhs=codes[rhs][:, PACK * rhs_col : PACK * (rhs_col + n)].bitcast(FP8X4),
+                rhs_scale=scales[rhs][:, rhs_col : rhs_col + n],
                 start=start,
                 stop=stop,
             )
 
         tensor_work = {}
+        passes_done = {}
 
         def transposes(i, q):
             def run(bank):
-                w = raws["x", i][:].bitcast(F32)
-                xt = bank[:].rearrange("p (g u r) -> p g u r", g=2, u=2)
+                words = raw["x%d" % i][:].bitcast(F32)
+                turned = bank[:].rearrange("p (g u m) -> p g u m", g=2, u=2)
                 for j in range(2):
-                    base = 256 * (2 * q + j)
+                    first = 2 * P * (2 * q + j)
                     for u in range(2):
-                        nc.tensor.transpose(xt[:, j, u, :], w[:, base + u : base + 256 : 2], ident[:])
+                        nc.tensor.transpose(
+                            turned[:, j, u, :], words[:, first + u : first + 2 * P : 2], identity[:]
+                        )
+
             return run
 
-        count = {}
-
-        def pass_of(key, total, cols, lhs, lcol, rhs, rcol, n):
+        def one_pass(group, passes, col, lhs, lhs_col, rhs, n):
             def run(bank):
-                done = count.get(key, 0)
-                count[key] = done + 1
-                mm(bank[:, cols : cols + n], lhs, lcol, rhs, rcol, n, done == 0, done == total - 1)
+                done = passes_done.get(group, 0)
+                passes_done[group] = done + 1
+                multiply(bank[:, col : col + n], lhs, lhs_col, rhs, 0, n, done == 0, done == passes - 1)
+
             return run
 
-        def passes4(i, cb):
+        def key_columns(i, n):
             def run(bank):
+                col = P * (i % PACK)
                 for k in range(D_PASSES):
-                    mm(
-                        bank[:, P * (i % PACK) : P * (i % PACK + 1)],
-                        "x%d" % i, P * k, "wk%d" % k, P * cb, P, k == 0, k == D_PASSES - 1,
+                    multiply(
+                        bank[:, col : col + P], "x%d" % i, P * k, "wk%d" % k, P * n, P, k == 0, k == D_PASSES - 1
                     )
+
             return run
 
-        for i in range(8):
+        for i in range(X_TILES):
             for q in range(2):
-                tensor_work["xT%d%d" % (i, q)] = (0, "x%d%d" % (i, q), ["x%d.load" % i if i else "x0%s.load" % "ab"[q]], transposes(i, q))
-        for i in range(4):
-            for k in range(4):
-                tensor_work["kM%d%d" % (i, k)] = (
-                    1, "k%d" % i, ["x%d" % i, "wk%d" % k],
-                    pass_of("k%d" % i, 4, 0, "x%d" % i, P * k, "wk%d" % k, 0, R),
+                needs = ["x0" + "ab"[q] if i == 0 else "load x%d" % i]
+                tensor_work["turn %d %d" % (i, q)] = (0, "x%d%d" % (i, q), needs, transposes(i, q))
+        for i in range(PACK):
+            for k in range(D_PASSES):
+                tensor_work["key %d %d" % (i, k)] = (
+                    1, "key %d" % i, ["x%d" % i, "wk%d" % k],
+                    one_pass("key %d" % i, D_PASSES, 0, "x%d" % i, P * k, "wk%d" % k, R),
                 )
-        for i in range(4, 8):
-            for cb in range(4):
-                tensor_work["kN%d%d" % (i, cb)] = (
-                    1, "n1%d" % cb, ["x%d" % i] + ["wk%d" % k for k in range(4)], passes4(i, cb),
-                )
+        for i in range(PACK, X_TILES):
+            for n in range(R // P):
+                needs = ["x%d" % i] + ["wk%d" % k for k in range(D_PASSES)]
+                tensor_work["key columns %d %d" % (i, n)] = (1, "key columns %d" % n, needs, key_columns(i, n))
         for h in range(2):
-            for i in range(8):
-                for k in range(4):
-                    w = "wv%d%d" % (k, h)
-                    b = "ad"[h]
-                    tensor_work["vM%d%s%d" % (i, b, k)] = (
-                        2 + h, "v%d%s" % (i, b), ["x%d" % i, w],
-                        pass_of("v%d%s" % (i, b), 4, 0, "x%d" % i, P * k, w, 0, HALF),
+            for i in range(X_TILES):
+                for k in range(D_PASSES):
+                    bank, weights = "val %d %d" % (i, h), "wv%d%d" % (k, h)
+                    tensor_work["val %d %d %d" % (i, h, k)] = (
+                        2 + h, bank, ["x%d" % i, weights],
+                        one_pass(bank, D_PASSES, 0, "x%d" % i, P * k, weights, BANK),
                     )
-        for b, rank in (("a", 4), ("b", 6), ("c", 7)):
+        for rank, b in enumerate("abc"):
             n = BLOCKS[b][1]
-            for m in range(4):
-                for g in range(2):
-                    pair = m % 2 if b == "b" else 0
+            for m in range(M_TILES):
+                second = m % 2 if b == "b" else 0
+                for g in range(GROUPS):
                     needs = ["key%d" % g, "val%d%s" % (g, b)]
-                    if pair:
-                        needs += ["oM%db0" % (m - 1), "oM%db1" % (m - 1)]
-                    tensor_work["oM%d%s%d" % (m, b, g)] = (
-                        rank, "o%d%s" % (m - pair, b), needs,
-                        pass_of("o%d%s" % (m, b), 2, n * pair, "key%d" % g, P * m, "val%d%s" % (g, b), 0, n),
+                    if second:
+                        needs += ["out %d b %d" % (m - 1, j) for j in range(GROUPS)]
+                    tensor_work["out %d %s %d" % (m, b, g)] = (
+                        4 + rank, "out %d %s" % (m - second, b), needs,
+                        one_pass("out %d %s" % (m, b), GROUPS, n * second, "key%d" % g, P * m, "val%d%s" % (g, b), n),
                     )
 
-        ready = set()
-        free_banks = list(range(8))
-        state = {"tiles": 0, "transposed": 0, "run": 0, "matmuls": 0}
+        issued = set()
         pending = []
+        banks = {}
+        free_banks = list(range(BANKS))
+        count = {"turning": 0, "turned": 0}
 
-        def announce(key):
-            ready.add(key)
-            for name, (rank, bank, needs, run) in tensor_work.items():
-                if key in needs and all(k in ready for k in needs):
+        def announce(name):
+            issued.add(name)
+            for job, (rank, bank, needs, run) in tensor_work.items():
+                if name in needs and all(k in issued for k in needs):
                     at = len(pending)
                     while at > 0 and tensor_work[pending[at - 1]][0] > rank:
                         at -= 1
-                    pending[at:at] = [name]
+                    pending[at:at] = [job]
 
-        def warm(bank):
-            nc.tensor.matmul(bank[:], zeros[:, :P], zeros[:, P:], start=True, stop=True)
+        def may_open(rank):
+            if len(free_banks) == 0:
+                return False
+            if rank == 0:
+                return count["turning"] < 4
+            return len(free_banks) > 2 or count["turned"] == 2 * X_TILES
 
-        def take(matmuls_only):
-            for name in list(pending):
-                rank, key, needs, run = tensor_work[name]
-                if rank == 0 and matmuls_only:
-                    continue
+        def issue_one():
+            for job in list(pending):
+                rank, key, needs, run = tensor_work[job]
                 if key not in banks:
-                    if len(free_banks) == 0:
-                        continue
-                    if rank == 0:
-                        if state["tiles"] >= 4:
-                            continue
-                        state["tiles"] += 1
-                    elif len(free_banks) <= 2 and state["transposed"] < 16:
+                    if not may_open(rank):
                         continue
                     b = free_banks.pop(0)
-                    banks[key] = (b, psum.tile([P, 512], F32, name="bank", tag="bank%d" % b, bufs=1))
-                if rank == 0:
-                    for turn in range(WARM_UP if state["transposed"] == 0 else int(state["run"] >= RUN_MAX)):
-                        warm(banks[key][1])
-                        state["run"] = 0
-                    state["transposed"] += 1
-                    state["run"] += 4
-                    state["matmuls"] = 0
-                else:
-                    state["run"] = 0
-                    state["matmuls"] += 1
+                    banks[key] = (b, psum.tile([P, BANK], F32, name="bank", tag="bank%d" % b, bufs=1))
+                    count["turning"] += int(rank == 0)
+                count["turned"] += int(rank == 0)
                 run(banks[key][1])
-                pending.remove(name)
-                announce(name)
+                pending.remove(job)
+                announce(job)
                 return True
             return False
 
-        def flush():
-            again = True
-            while again:
-                first = state["run"] >= RUN_MAX or (state["run"] == 0 and state["matmuls"] < MM_RUN)
-                again = (first and take(True)) or take(False)
+        def bank_of(key):
+            return banks[key][1]
 
-        def release(key):
+        def free_bank(key):
             free_banks.append(banks[key][0])
             banks.pop(key)
-            if key[0] == "x":
-                state["tiles"] -= 1
 
-        def row_tile(key, n):
+        rows = {}
+
+        def copy(engine, dst, src):
+            if engine == "S":
+                nc.scalar.copy(out=dst, in_=src)
+            else:
+                nc.vector.tensor_copy(out=dst, in_=src)
+
+        def times(engine, dst, src, factor):
+            if engine == "S":
+                nc.scalar.activation(out=dst, in_=src, func=COPY, scale=factor)
+            else:
+                nc.vector.tensor_scalar(out=dst, in0=src, scalar1=factor, scalar2=None, op0=MULT)
+
+        def words(engine, i, q):
+            key = "x%d" % i
+            if key not in source:
+                source[key] = slot([P, PASS * PACK])
+            half = BANK * 2
+            dst = source[key][:, half * q : half * (q + 1)].bitcast(F32)
+            copy(
+                engine,
+                dst.rearrange("p (g m u) -> p g m u", g=2, u=2),
+                bank_of("x%d%d" % (i, q))[:].rearrange("p (g u m) -> p g m u", g=2, u=2),
+            )
+            count["turning"] -= 1
+            free_bank("x%d%d" % (i, q))
+
+        def widen(engine, g, q):
+            key = "wv%d" % g
             if key not in rows:
-                rows[key] = work.tile(
-                    [P, PACK, n], BF16, name="rows", tag="t4" if n == 512 else "t2",
-                    bufs=T4 if n == 512 else 4, align_bytes=64,
-                )
-            return rows[key]
+                rows[key] = work.tile([P, PACK, C], BF16, name="wide", tag="wide", bufs=D_PASSES, align_bytes=64)
+            for t in (2 * q, 2 * q + 1):
+                times(engine, rows[key][:, t, :], raw[key][:, t, :].bitcast(FP8), wv_scale[:, g, t : t + 1])
 
-        def unit(name, engine):
-            kind, arg = name[:3], name[3:]
-            if name[:2] == "xC":
-                i, q = int(name[2]), int(name[3])
-                if q == 0 and "x%d" % i not in ils or q == 1 and "x%d" % i not in ils:
-                    il_tile("x%d" % i, 512)
-                bank = banks["x%d%d" % (i, q)][1]
-                dst = ils["x%d" % i][:, 1024 * q : 1024 * (q + 1)].bitcast(F32)
-                dst = dst.rearrange("p (g r u) -> p g r u", g=2, u=2)
-                src = bank[:].rearrange("p (g u r) -> p g r u", g=2, u=2)
-                if engine == "S":
-                    nc.scalar.copy(out=dst, in_=src)
-                else:
-                    nc.vector.tensor_copy(out=dst, in_=src)
-                release("x%d%d" % (i, q))
-            elif name[:2] == "xQ":
-                quantize("x" + name[2])
-                announce("x" + name[2])
-            elif kind == "wkI":
-                interleave("wk" + arg, raws["wk", int(arg)][:], engine)
-            elif kind == "wkQ":
-                quantize("wk" + arg)
-                announce("wk" + arg)
-            elif kind == "wvW":
-                g, p = int(arg[0]), int(arg[1])
-                if "w%d" % g not in rows:
-                    rows["w%d" % g] = work.tile([P, PACK, C], BF16, name="wide", tag="wide", bufs=4, align_bytes=64)
-                for t in (2 * p, 2 * p + 1):
-                    scaled(
-                        rows["w%d" % g][:, t, :], raws["wv", g][:, t, :].bitcast(FP8),
-                        wv_scale[:, g, t : t + 1], engine,
-                    )
-            elif kind == "wvI":
-                h = int(arg[1])
-                interleave("wv" + arg, rows["w" + arg[0]][:, :, HALF * h : HALF * (h + 1)], engine)
-            elif kind == "wvQ":
-                quantize("wv" + arg)
-                announce("wv" + arg)
-            elif name[:2] == "kA" and len(name) == 3:
-                i = int(name[2])
-                nc.vector.tensor_tensor(
-                    out=row_tile("k%d" % (i // PACK), 512)[:, i % PACK, :], in0=banks["k%d" % i][1][:],
-                    in1=raws["pos", i // PACK][:, i % PACK, :], op=ALU.add,
-                )
-                release("k%d" % i)
-            elif name[:2] == "kA":
-                g, cb = int(name[2]), int(name[4])
-                if "sum%d" % g not in rows:
-                    rows["sum%d" % g] = work.tile([P, R * PACK], BF16, name="ksum", tag="t4", bufs=T4, align_bytes=64)
-                nc.vector.tensor_tensor(
-                    out=rows["sum%d" % g][:, 512 * cb : 512 * (cb + 1)].rearrange("p (c t) -> p c t", t=PACK),
-                    in0=banks["n%d%d" % (g, cb)][1][:].rearrange("p (t c) -> p c t", t=PACK),
-                    in1=raws["pos", g][:, :, P * cb : P * (cb + 1)].rearrange("p t c -> p c t"),
-                    op=ALU.add,
-                )
-                release("n%d%d" % (g, cb))
-            elif name == "kI0":
-                interleave("key0", rows["k0"][:], engine, relu=True)
-            elif name == "kI1":
-                nc.vector.tensor_scalar(
-                    out=il_tile("key1", 512)[:], in0=rows["sum1"][:], scalar1=0.0, scalar2=None, op0=ALU.max
-                )
-            elif name[:2] == "kQ":
-                quantize("key" + name[2])
-                announce("key" + name[2])
-            elif name[:2] == "vO":
-                i, b = int(name[2]), name[3]
-                scaled(
-                    row_tile("v%d%s" % (i // PACK, b), HALF)[:, i % PACK, :], banks["v%d%s" % (i, b)][1][:],
-                    emph[:, i // PACK, i % PACK : i % PACK + 1], engine,
-                )
-                release("v%d%s" % (i, b))
-            elif name[:2] == "vI":
-                g, b = name[2], name[3]
-                src = rows["v" + g + ("a" if b == "a" else "d")]
-                cut = slice(0, HALF) if b == "a" else slice(BLOCKS[b][0] - HALF, BLOCKS[b][0] - HALF + BLOCKS[b][1])
-                interleave("val" + name[2:], src[:, :, cut], engine, n=BLOCKS[b][1])
-            elif name[:2] == "vQ":
-                quantize("val" + name[2:])
-                announce("val" + name[2:])
-            elif name[:2] == "oC":
-                m, b = int(name[2]), name[3]
-                c0, n = BLOCKS[b]
-                rows_m = 2 if b == "b" else 1
-                w = n * rows_m
-                res = work.tile([P, w], F32, name="res", tag="res%d" % w, bufs=6 if w == 512 else 4)
-                bank = banks["o%d%s" % (m, b)][1]
-                if engine == "S":
-                    nc.scalar.copy(out=res[:], in_=bank[:, :w])
-                else:
-                    nc.vector.tensor_copy(out=res[:], in_=bank[:, :w])
-                release("o%d%s" % (m, b))
-                nc.sync.dma_start(
-                    out=out[P * m : P * (m + rows_m), c0 : c0 + n].rearrange("(m p) c -> p m c", p=P),
-                    in_=res[:].rearrange("p (m c) -> p m c", c=n),
-                )
+        def interleave(engine, key):
+            n = BANK
+            if key[:2] == "wk":
+                src = raw[key][:]
+            elif key[:2] == "wv":
+                h = int(key[3])
+                src = rows[key[:3]][:, :, BANK * h : BANK * (h + 1)]
+            elif key == "key1":
+                source[key] = slot([P, R * PACK])
+                nc.vector.tensor_scalar(out=source[key][:], in0=rows[key][:], scalar1=0.0, scalar2=None, op0=MAX)
+                return
+            elif key == "key0":
+                src = rows[key][:]
+            else:
+                first, n = BLOCKS[key[4]]
+                first = first % BANK
+                src = rows["val" + key[3] + str(BLOCKS[key[4]][0] // BANK)][:, :, first : first + n]
+            if n == BANK:
+                source[key] = slot([P, n * PACK])
+            else:
+                source[key] = work.tile([P, n * PACK], BF16, name="narrow", tag="narrow", bufs=4, align_bytes=64)
+            dst = source[key][:].rearrange("p (c i t) -> p c t i", i=4, t=PACK)
+            src = src.rearrange("p t (c i) -> p c t i", i=4)
+            if key != "key0":
+                copy(engine, dst, src)
+            elif engine == "S":
+                nc.scalar.activation(out=dst, in_=src, func=RELU)
+            else:
+                nc.vector.tensor_scalar(out=dst, in0=src, scalar1=0.0, scalar2=None, op0=MAX)
 
-        for word in words:
-            if word[0] == "x":
-                announce(word + ".load")
-        flush()
-        for at, word in enumerate(ORDER.split()):
-            name, engine = word.split(".")
-            if at == 8:
-                nc.vector.tensor_copy(out=emph[:], in_=emph_bf[:])
-            unit(name, engine)
-            flush()
+        def add_pos(i):
+            if "key0" not in rows:
+                rows["key0"] = slot([P, PACK, R])
+            nc.vector.tensor_tensor(
+                out=rows["key0"][:, i, :], in0=bank_of("key %d" % i)[:], in1=raw["pos0"][:, i, :], op=ADD
+            )
+            free_bank("key %d" % i)
+
+        def add_pos_columns(n):
+            if "key1" not in rows:
+                rows["key1"] = slot([P, R * PACK])
+            nc.vector.tensor_tensor(
+                out=rows["key1"][:, BANK * n : BANK * (n + 1)].rearrange("p (c t) -> p c t", t=PACK),
+                in0=bank_of("key columns %d" % n)[:].rearrange("p (t c) -> p c t", t=PACK),
+                in1=raw["pos1"][:, :, P * n : P * (n + 1)].rearrange("p t c -> p c t"),
+                op=ADD,
+            )
+            free_bank("key columns %d" % n)
+
+        def times_emphasis(engine, i, h):
+            g, t = i // PACK, i % PACK
+            key = "val%d%d" % (g, h)
+            if key not in rows:
+                rows[key] = slot([P, PACK, BANK])
+            times(engine, rows[key][:, t, :], bank_of("val %d %d" % (i, h))[:], emphasis_f32[:, g, t : t + 1])
+            free_bank("val %d %d" % (i, h))
+
+        def store_out(engine, m, b):
+            first, n = BLOCKS[b]
+            tiles = 2 if b == "b" else 1
+            width = n * tiles
+            res = work.tile([P, width], F32, name="res", tag="res%d" % width, bufs=6 if width == BANK else 4)
+            key = "out %d %s" % (m, b)
+            copy(engine, res[:], bank_of(key)[:, :width])
+            free_bank(key)
+            nc.sync.dma_start(
+                out=out[P * m : P * (m + tiles), first : first + n].rearrange("(j p) c -> p j c", p=P),
+                in_=res[:].rearrange("p (j c) -> p j c", c=n),
+            )
+
+        for word in LOADS.split():
+            announce(word if word[:2] == "x0" else "load " + word)
+        while issue_one():
+            pass
+        for step in ORDER.split():
+            name, engine = step.split("@")
+            kind = name.split(".")[0]
+            args = name.split(".")[1:]
+            if kind == "factors":
+                nc.vector.tensor_copy(out=emphasis_f32[:], in_=emphasis_bf[:])
+            elif kind == "words":
+                words(engine, int(args[0]), int(args[1]))
+            elif kind == "widen":
+                widen(engine, int(args[0]), int(args[1]))
+            elif kind == "interleave":
+                interleave(engine, args[0])
+            elif kind == "quantize":
+                quantize(args[0])
+                announce(args[0])
+            elif kind == "pos" and len(args) == 1:
+                add_pos(int(args[0]))
+            elif kind == "pos":
+                add_pos_columns(int(args[1]))
+            elif kind == "emphasis":
+                times_emphasis(engine, int(args[0]), int(args[1]))
+            else:
+                store_out(engine, int(args[0]), args[1])
+            while issue_one():
+                pass

from contextlib import ExitStack

import concourse.mybir as mybir
from concourse.masks import make_identity

T, D, R, C = 1024, 2048, 512, 1024
FLOPS = 2 * T * D * (R + C) + 2 * T * R * C

F32 = mybir.dt.float32
BF16 = mybir.dt.bfloat16
U8 = mybir.dt.uint8
FP8 = mybir.dt.float8_e4m3fn
FP8X4 = mybir.dt.float8_e4m3fn_x4
ADD = mybir.AluOpType.add
MAX = mybir.AluOpType.max
MULT = mybir.AluOpType.mult
COPY = mybir.ActivationFunctionType.Copy
RELU = mybir.ActivationFunctionType.Relu

P = 128
PACK = 4
PASS = P * PACK
D_PASSES = D // PASS
GROUPS = T // PASS
X_TILES = T // P
M_TILES = R // P
BANK = 512
BANKS = 8

BLOCKS = {"a": (0, 512), "b": (512, 256), "c": (768, 256)}

SLOTS = 22

LOADS = "wv0a wv2 wv3 x0a wv0b x0b x3 x6 x1 x7 x4 x2 x5 wv1 pos1 wk3 wk2 wk0 wk1 pos0"

ORDER = """
    factors@V widen.0.0@V widen.2.1@V widen.3.0@V widen.2.0@S interleave.wv20@V widen.3.1@S
    words.0.0@V widen.0.1@S quantize.wv20@V words.3.0@S words.0.1@S words.6.0@S words.6.1@S
    interleave.wv31@V interleave.wv30@V interleave.wv00@V words.7.0@S words.7.1@S words.4.0@S
    words.4.1@S words.2.0@S words.1.1@S words.1.0@S quantize.x0@V quantize.wv30@V words.3.1@S
    quantize.wv00@V quantize.x6@V quantize.x7@V words.5.1@S quantize.x4@V widen.1.1@V widen.1.0@V
    quantize.x1@V words.5.0@S words.2.1@S quantize.x5@V interleave.wv10@S interleave.wk3@S
    quantize.x2@V quantize.x3@V interleave.wk2@V quantize.wv10@V interleave.wk1@V emphasis.1.0@S
    quantize.wk2@V quantize.wk3@V emphasis.2.0@S quantize.wk1@V quantize.wv31@V emphasis.3.0@S
    emphasis.4.0@S emphasis.5.0@S emphasis.0.0@V interleave.wk0@V quantize.wk0@V interleave.wv01@S
    emphasis.6.0@S emphasis.7.0@V pos.1@V quantize.wv01@V interleave.wv21@S pos.0@V pos.3@V
    quantize.wv21@V interleave.wv11@V pos.2@V interleave.val0a@V quantize.wv11@V quantize.val0a@V
    pos.1.2@V interleave.key0@S pos.1.0@V interleave.val1a@S pos.1.3@V quantize.key0@V
    quantize.val1a@V pos.1.1@V emphasis.2.1@V emphasis.5.1@S interleave.key1@V quantize.key1@V
    emphasis.1.1@V emphasis.0.1@S emphasis.6.1@S emphasis.3.1@S emphasis.4.1@V emphasis.7.1@S
    interleave.val0b@V interleave.val1b@V store.0.a@S quantize.val0b@V store.1.a@S store.2.a@S
    quantize.val1b@V store.3.a@S interleave.val1c@V interleave.val0c@V quantize.val1c@V
    store.0.b@S quantize.val0c@V store.2.b@V store.0.c@V store.1.c@S store.2.c@S store.3.c@V
"""


def tile_text_image_memory_bridge_s7_kernel(
    tc, x, w_key, w_value_bytes, w_value_scale, pos, emphasis, out
):
    nc = tc.nc
    with ExitStack() as ctx:
        work = ctx.enter_context(tc.tile_pool(name="work", bufs=1))
        keep = ctx.enter_context(tc.tile_pool(name="keep", bufs=1))
        psum = ctx.enter_context(tc.psum_pool(name="psum", bufs=1))
        ctx.enter_context(tc.manual_schedule())

        def slot(shape):
            return work.tile(shape, BF16, name="slot", tag="slot", bufs=SLOTS, align_bytes=64)

        views = {
            "x": x.rearrange("(g p t) k -> g t p k", p=P, t=PACK),
            "wk": w_key.rearrange("(g p t) n -> g p t n", p=P, t=PACK),
            "wv": w_value_bytes.rearrange("(g p t) n -> g p t n", p=P, t=PACK),
            "pos": pos.rearrange("(g p t) n -> g p t n", p=P, t=PACK),
        }
        raw = {}

        def raw_tile(kind):
            if kind == "x":
                return slot([P, D])
            if kind == "wk":
                return slot([P, PACK, R])
            if kind == "wv":
                return work.tile([P, PACK, C], U8, name="bytes", tag="bytes", bufs=D_PASSES, align_bytes=64)
            return work.tile([P, PACK, R], BF16, name="pos", tag="pos", bufs=GROUPS, align_bytes=64)

        def load(word):
            half = word[-1] if word[-1] in "ab" else ""
            key = word[:-1] if half else word
            kind, n = key[:-1], int(key[-1])
            if key not in raw:
                raw[key] = raw_tile(kind)
            source = views["x"][n // PACK, n % PACK] if kind == "x" else views[kind][n]
            extent = D if kind == "x" else PACK
            cut = slice(0, extent)
            if half == "a":
                cut = slice(0, extent // 2)
            elif half == "b":
                cut = slice(extent // 2, extent)
            nc.sync.dma_start(out=raw[key][:, cut], in_=source[:, cut])

        wv_scale = keep.tile([P, D_PASSES, PACK], F32, name="wv_scale")
        nc.scalar.dma_start(
            out=wv_scale[:], in_=w_value_scale.rearrange("(g p t) o -> p g (t o)", p=P, t=PACK)
        )
        emphasis_bf = keep.tile([P, GROUPS, PACK], BF16, name="emphasis_bf")
        nc.scalar.dma_start(out=emphasis_bf[:], in_=emphasis.rearrange("(g p t) -> p g t", p=P, t=PACK))
        table = keep.tile([P, 1], F32, name="table")
        nc.vector.memset(table[:], 0.0)
        nc.scalar.activation(out=table[:], in_=table[:], func=COPY)
        for word in LOADS.split():
            load(word)
        identity = keep.tile([P, P], F32, name="identity")
        make_identity(nc, identity[:])
        emphasis_f32 = keep.tile([P, GROUPS, PACK], F32, name="emphasis_f32")

        s_words = X_TILES * PASS + GROUPS * R
        m_words = D_PASSES * (R + C) + GROUPS * C
        store = {}
        for kind, each, words, start in (
            ("stationary", PACK, s_words, 0),
            ("moving", PACK, m_words, 64),
            ("stationary", 1, s_words, 128),
            ("moving", 1, m_words, 192),
        ):
            tile = keep.tile([P, 256 + each * words], U8, name="store_%s%d" % (kind, each), align_bytes=256)
            store[kind, each] = (tile, [start])

        def store_bytes(kind, each, words):
            tile, ends = store[kind, each]
            ends.append(ends[-1] + each * words)
            return tile[:, ends[-2] : ends[-1]]

        source, codes, scales = {}, {}, {}

        def quantize(key):
            values = source[key][:]
            words = values.shape[1] // PACK
            kind = "stationary" if key[0] in "xk" else "moving"
            codes[key] = store_bytes(kind, PACK, words)
            scales[key] = store_bytes(kind, 1, words)
            nc.vector.quantize_mx(out=codes[key].bitcast(FP8X4), scales=scales[key], in_=values)

        def multiply(bank, lhs, lhs_col, rhs, rhs_col, n, start, stop):
            nc.tensor.matmul_mx(
                out=bank,
                lhsT=codes[lhs][:, PACK * lhs_col : PACK * (lhs_col + P)].bitcast(FP8X4),
                lhsT_scale=scales[lhs][:, lhs_col : lhs_col + P],
                rhs=codes[rhs][:, PACK * rhs_col : PACK * (rhs_col + n)].bitcast(FP8X4),
                rhs_scale=scales[rhs][:, rhs_col : rhs_col + n],
                start=start,
                stop=stop,
            )

        tensor_work = {}
        passes_done = {}

        def transposes(i, q):
            def run(bank):
                words = raw["x%d" % i][:].bitcast(F32)
                turned = bank[:].rearrange("p (g u m) -> p g u m", g=2, u=2)
                for j in range(2):
                    first = 2 * P * (2 * q + j)
                    for u in range(2):
                        nc.tensor.transpose(
                            turned[:, j, u, :], words[:, first + u : first + 2 * P : 2], identity[:]
                        )

            return run

        def one_pass(group, passes, col, lhs, lhs_col, rhs, n):
            def run(bank):
                done = passes_done.get(group, 0)
                passes_done[group] = done + 1
                multiply(bank[:, col : col + n], lhs, lhs_col, rhs, 0, n, done == 0, done == passes - 1)

            return run

        def key_columns(i, n):
            def run(bank):
                col = P * (i % PACK)
                for k in range(D_PASSES):
                    multiply(
                        bank[:, col : col + P], "x%d" % i, P * k, "wk%d" % k, P * n, P, k == 0, k == D_PASSES - 1
                    )

            return run

        for i in range(X_TILES):
            for q in range(2):
                needs = ["x0" + "ab"[q] if i == 0 else "load x%d" % i]
                tensor_work["turn %d %d" % (i, q)] = (0, "x%d%d" % (i, q), needs, transposes(i, q))
        for i in range(PACK):
            for k in range(D_PASSES):
                tensor_work["key %d %d" % (i, k)] = (
                    1, "key %d" % i, ["x%d" % i, "wk%d" % k],
                    one_pass("key %d" % i, D_PASSES, 0, "x%d" % i, P * k, "wk%d" % k, R),
                )
        for i in range(PACK, X_TILES):
            for n in range(R // P):
                needs = ["x%d" % i] + ["wk%d" % k for k in range(D_PASSES)]
                tensor_work["key columns %d %d" % (i, n)] = (1, "key columns %d" % n, needs, key_columns(i, n))
        for h in range(2):
            for i in range(X_TILES):
                for k in range(D_PASSES):
                    bank, weights = "val %d %d" % (i, h), "wv%d%d" % (k, h)
                    tensor_work["val %d %d %d" % (i, h, k)] = (
                        2 + h, bank, ["x%d" % i, weights],
                        one_pass(bank, D_PASSES, 0, "x%d" % i, P * k, weights, BANK),
                    )
        for rank, b in enumerate("abc"):
            n = BLOCKS[b][1]
            for m in range(M_TILES):
                second = m % 2 if b == "b" else 0
                for g in range(GROUPS):
                    needs = ["key%d" % g, "val%d%s" % (g, b)]
                    if second:
                        needs += ["out %d b %d" % (m - 1, j) for j in range(GROUPS)]
                    tensor_work["out %d %s %d" % (m, b, g)] = (
                        4 + rank, "out %d %s" % (m - second, b), needs,
                        one_pass("out %d %s" % (m, b), GROUPS, n * second, "key%d" % g, P * m, "val%d%s" % (g, b), n),
                    )

        issued = set()
        pending = []
        banks = {}
        free_banks = list(range(BANKS))
        count = {"turning": 0, "turned": 0}

        def announce(name):
            issued.add(name)
            for job, (rank, bank, needs, run) in tensor_work.items():
                if name in needs and all(k in issued for k in needs):
                    at = len(pending)
                    while at > 0 and tensor_work[pending[at - 1]][0] > rank:
                        at -= 1
                    pending[at:at] = [job]

        def may_open(rank):
            if len(free_banks) == 0:
                return False
            if rank == 0:
                return count["turning"] < 4
            return len(free_banks) > 2 or count["turned"] == 2 * X_TILES

        def issue_one():
            for job in list(pending):
                rank, key, needs, run = tensor_work[job]
                if key not in banks:
                    if not may_open(rank):
                        continue
                    b = free_banks.pop(0)
                    banks[key] = (b, psum.tile([P, BANK], F32, name="bank", tag="bank%d" % b, bufs=1))
                    count["turning"] += int(rank == 0)
                count["turned"] += int(rank == 0)
                run(banks[key][1])
                pending.remove(job)
                announce(job)
                return True
            return False

        def bank_of(key):
            return banks[key][1]

        def free_bank(key):
            free_banks.append(banks[key][0])
            banks.pop(key)

        rows = {}

        def copy(engine, dst, src):
            if engine == "S":
                nc.scalar.copy(out=dst, in_=src)
            else:
                nc.vector.tensor_copy(out=dst, in_=src)

        def times(engine, dst, src, factor):
            if engine == "S":
                nc.scalar.activation(out=dst, in_=src, func=COPY, scale=factor)
            else:
                nc.vector.tensor_scalar(out=dst, in0=src, scalar1=factor, scalar2=None, op0=MULT)

        def words(engine, i, q):
            key = "x%d" % i
            if key not in source:
                source[key] = slot([P, PASS * PACK])
            half = BANK * 2
            dst = source[key][:, half * q : half * (q + 1)].bitcast(F32)
            copy(
                engine,
                dst.rearrange("p (g m u) -> p g m u", g=2, u=2),
                bank_of("x%d%d" % (i, q))[:].rearrange("p (g u m) -> p g m u", g=2, u=2),
            )
            count["turning"] -= 1
            free_bank("x%d%d" % (i, q))

        def widen(engine, g, q):
            key = "wv%d" % g
            if key not in rows:
                rows[key] = work.tile([P, PACK, C], BF16, name="wide", tag="wide", bufs=D_PASSES, align_bytes=64)
            for t in (2 * q, 2 * q + 1):
                times(engine, rows[key][:, t, :], raw[key][:, t, :].bitcast(FP8), wv_scale[:, g, t : t + 1])

        def interleave(engine, key):
            n = BANK
            if key[:2] == "wk":
                src = raw[key][:]
            elif key[:2] == "wv":
                h = int(key[3])
                src = rows[key[:3]][:, :, BANK * h : BANK * (h + 1)]
            elif key == "key1":
                source[key] = slot([P, R * PACK])
                nc.vector.tensor_scalar(out=source[key][:], in0=rows[key][:], scalar1=0.0, scalar2=None, op0=MAX)
                return
            elif key == "key0":
                src = rows[key][:]
            else:
                first, n = BLOCKS[key[4]]
                first = first % BANK
                src = rows["val" + key[3] + str(BLOCKS[key[4]][0] // BANK)][:, :, first : first + n]
            if n == BANK:
                source[key] = slot([P, n * PACK])
            else:
                source[key] = work.tile([P, n * PACK], BF16, name="narrow", tag="narrow", bufs=4, align_bytes=64)
            dst = source[key][:].rearrange("p (c i t) -> p c t i", i=4, t=PACK)
            src = src.rearrange("p t (c i) -> p c t i", i=4)
            if key != "key0":
                copy(engine, dst, src)
            elif engine == "S":
                nc.scalar.activation(out=dst, in_=src, func=RELU)
            else:
                nc.vector.tensor_scalar(out=dst, in0=src, scalar1=0.0, scalar2=None, op0=MAX)

        def add_pos(i):
            if "key0" not in rows:
                rows["key0"] = slot([P, PACK, R])
            nc.vector.tensor_tensor(
                out=rows["key0"][:, i, :], in0=bank_of("key %d" % i)[:], in1=raw["pos0"][:, i, :], op=ADD
            )
            free_bank("key %d" % i)

        def add_pos_columns(n):
            if "key1" not in rows:
                rows["key1"] = slot([P, R * PACK])
            nc.vector.tensor_tensor(
                out=rows["key1"][:, BANK * n : BANK * (n + 1)].rearrange("p (c t) -> p c t", t=PACK),
                in0=bank_of("key columns %d" % n)[:].rearrange("p (t c) -> p c t", t=PACK),
                in1=raw["pos1"][:, :, P * n : P * (n + 1)].rearrange("p t c -> p c t"),
                op=ADD,
            )
            free_bank("key columns %d" % n)

        def times_emphasis(engine, i, h):
            g, t = i // PACK, i % PACK
            key = "val%d%d" % (g, h)
            if key not in rows:
                rows[key] = slot([P, PACK, BANK])
            times(engine, rows[key][:, t, :], bank_of("val %d %d" % (i, h))[:], emphasis_f32[:, g, t : t + 1])
            free_bank("val %d %d" % (i, h))

        def store_out(engine, m, b):
            first, n = BLOCKS[b]
            tiles = 2 if b == "b" else 1
            width = n * tiles
            res = work.tile([P, width], F32, name="res", tag="res%d" % width, bufs=6 if width == BANK else 4)
            key = "out %d %s" % (m, b)
            copy(engine, res[:], bank_of(key)[:, :width])
            free_bank(key)
            nc.sync.dma_start(
                out=out[P * m : P * (m + tiles), first : first + n].rearrange("(j p) c -> p j c", p=P),
                in_=res[:].rearrange("p (j c) -> p j c", c=n),
            )

        for word in LOADS.split():
            announce(word if word[:2] == "x0" else "load " + word)
        while issue_one():
            pass
        for step in ORDER.split():
            name, engine = step.split("@")
            kind = name.split(".")[0]
            args = name.split(".")[1:]
            if kind == "factors":
                nc.vector.tensor_copy(out=emphasis_f32[:], in_=emphasis_bf[:])
            elif kind == "words":
                words(engine, int(args[0]), int(args[1]))
            elif kind == "widen":
                widen(engine, int(args[0]), int(args[1]))
            elif kind == "interleave":
                interleave(engine, args[0])
            elif kind == "quantize":
                quantize(args[0])
                announce(args[0])
            elif kind == "pos" and len(args) == 1:
                add_pos(int(args[0]))
            elif kind == "pos":
                add_pos_columns(int(args[1]))
            elif kind == "emphasis":
                times_emphasis(engine, int(args[0]), int(args[1]))
            else:
                store_out(engine, int(args[0]), args[1])
            while issue_one():
                pass
